import numpy as np, ml_dtypes
CORES = [35,38,43,46]
N = 4
import mx_ref
BF = ml_dtypes.bfloat16
def gentries(a):
    return np.ascontiguousarray(a.reshape(8, 16, -1).transpose(0, 2, 1)).reshape(8, -1)
def gtable(e):
    e = np.asarray(e); return np.ascontiguousarray(e.reshape(8, -1, 16).transpose(0, 2, 1)).reshape(128, -1).astype(np.int32)
def gcols(t, e):
    v = np.concatenate([t.reshape(8, 16, -1, 4), np.zeros((8, 16, 1, 4), BF)], axis=2)
    return np.ascontiguousarray(np.stack([v[g][:, e[g]] for g in range(8)])).reshape(128, -1)
def tile(rs):
    return np.stack(rs, axis=2).reshape(128, -1).astype(BF)
def pick(q, e):
    c = np.concatenate([q[0].reshape(128, -1, 4), np.zeros((128, 1, 4), np.uint8)], axis=1); s = np.concatenate([q[1], np.ones((16, 1), np.uint8)], axis=1)
    return (np.ascontiguousarray(c[:, e].reshape(128, -1)), np.ascontiguousarray(s[:, e]))
def join(*qs):
    return (np.concatenate([q[0] for q in qs], axis=1), np.concatenate([q[1] for q in qs], axis=1))
def put(q, e, v):
    c, s = q[0].reshape(128, -1, 4).copy(), q[1].copy(); c[:, e] = v[0].reshape(128, -1, 4); s[:, e] = v[1]
    return (c.reshape(128, -1), s)
def pk(c, s):
    return (np.ascontiguousarray(c), mx_ref.live(s))
def emit(q):
    return q[0], q[1]
def packed(v, rng):
    q = [mx_ref.quantize(np.ascontiguousarray(v[r])) for r in range(N)]
    return np.stack([a for a, b in q]), np.stack([mx_ref.plane(b, rng) for a, b in q])
def values_of_codes():
    e, c = np.zeros((128, 128, 4), np.float32), np.zeros((128, 2, 4), np.uint8)
    e[np.arange(128), np.arange(128), 0] = 1
    c[:127, :, 0] = np.arange(256).reshape(2, 128).T[:127]
    return mx_ref.matmul(mx_ref.quantize(e.reshape(128, 512).astype(BF)), (c.reshape(128, 8), np.full((16, 2), 127, np.uint8))).T.reshape(-1).astype(np.float64)
CODE_VALUE, SCALE_VALUE = values_of_codes(), 2.0 ** (np.arange(256) - 127.0)
def decode(q):
    return (CODE_VALUE[q[0]].reshape(16, 8, -1, 4) * SCALE_VALUE[q[1]][:, None, :, None] + 0.0).reshape(128, -1).astype(np.float32)
def f(rng, *shape):
    return mx_ref.flush((rng.standard_normal(shape, dtype=np.float32) * np.exp2(rng.integers(-2, 3, shape[:-1] + (1,)))).astype(BF))
def wide(rng, *shape, cols=0):
    v = rng.standard_normal(shape, dtype=np.float32) * np.exp2(rng.integers(-12, 13, shape)).astype(np.float32)
    if cols: v *= np.repeat(np.exp2(rng.integers(-cols, cols + 1, shape[:-2] + (1, shape[-1] // 4))) * (rng.random(shape[:-2] + (1, shape[-1] // 4)) > 0.0625), 4, axis=-1).astype(np.float32)
    return mx_ref.flush(v.astype(BF))
C, H, R = 384, 128, 3
def numbers_of(rng):
    return {"x": np.array(f(rng, N, 128, 4 * C)), "u": np.array(f(rng, N, 128, 512)), "v": np.array(f(rng, N, 128, 512))}
def orders(rng):
    return np.argsort(rng.random((N, 8, C)), axis=2)
def bonds(e):
    return np.stack([gtable(e[r]) for r in range(N)])
def layers(rng, still=()):
    w = np.array(f(rng, N, 128, 2048)).reshape(N, 8, 16, 4, 8, 16, 4)
    for i in still:
        w[:, :, i] = 0
        w[:, :, :, :, :, i] = 0
    return w
def weights(rng, w):
    c, p = packed(np.ascontiguousarray(w).reshape(N, 128, 2048), rng)
    return {"wc": c, "ws": p}
def chosen(rng, n):
    k, a = np.arange(8 * n), np.zeros((8, C), bool)
    a[k % 8, k // 4] = True
    return a[:, rng.permutation(C)]
def crowd(rng):
    n, o = H + 1, rng.permutation(C)
    full, half, none, rest = o[:48], o[48:48 + n], o[48 + n:48 + 2 * n], o[48 + 2 * n:]
    a, e = np.zeros((8, C), bool), np.zeros((8, C), np.int64)
    a[:, full] = True
    for j in range(n): a[(j + 1 + rng.permutation(7)[:4]) % 8, half[j]] = True
    for g in range(8):
        b = np.concatenate([half[g::8], rng.permutation(np.delete(half, np.arange(g, n, 8)))])
        e[g, none] = rng.permutation(half)
        e[g, b[:48]] = rng.permutation(full)
        e[g, np.concatenate([b[48:], full])] = rng.permutation(none)
        e[g, rest] = rng.permutation(rest)
    return a, e
def faint():
    k = 2.0 ** -np.arange(4.0, 28.0)
    t = np.zeros((128, 24, 4), np.float32)
    t[0, :, 0] = 1.96875
    t[7, :, 0] = k
    once = decode(mx_ref.quantize(t.reshape(128, 96).astype(BF)))
    again = decode(mx_ref.quantize(once.astype(BF)))
    i = int(np.argmax((once[7, ::4] > 0) & (again[7, ::4] == 0)))
    assert once[7, 4 * i] == k[i] and again[7, 4 * i] == 0
    return k[i]
def plant(d, s):
    x = d["x"].reshape(N, 8, 16, C, 4)
    x[:, :, 0] = 0
    x[:, :, 0, :, 0] = s.astype(np.float32).astype(BF)
    u = d["u"].reshape(N, 128, 128, 4)
    u[:, :, ::16] = 0
    for h in range(0, 128, 16): u[:, h, h, 0] = 1
def setup_inputs(rng):
    return {**numbers_of(rng), "m": bonds(orders(rng)), **weights(rng, layers(rng))}
def setup_inputs_slots(rng):
    d = numbers_of(rng)
    e, s, c, h = orders(rng), np.zeros((N, 8, C)), int(rng.integers(4)), H // 2
    for r in range(N):
        k = (r + c) % 4
        if k == 0:
            a = chosen(rng, H)
            for g in rng.permutation(8)[:4]: a[g, rng.choice(np.flatnonzero(a[g]))] = False
        elif k == 1: a = chosen(rng, H + 1)
        elif k == 2:
            o = rng.permutation(C)
            a = np.zeros((8, C), bool)
            a[:, o[:h]] = True
            for g in range(8):
                e[r, g, o[h:2 * h]] = rng.permutation(o[:h])
                e[r, g, o[2 * h:3 * h]] = rng.permutation(o[h:2 * h])
                e[r, g, o[:h]] = rng.permutation(o[2 * h:3 * h])
                e[r, g, o[3 * h:]] = rng.permutation(o[3 * h:])
        else: a, e[r] = crowd(rng)
        s[r] = np.where(a, 1.0, -1.0 * rng.integers(0, 2, (8, C)))
    plant(d, s)
    x = d["x"].reshape(N, 8, 16, C, 4)
    x[:, :, 8:11] = 0
    x[:, :, 8, :, 0] = 1
    u = d["u"].reshape(N, 128, 128, 4)
    for i in range(0, 128, 16): u[:, i + 10, i, 0] = 1
    w, o = layers(rng, (0, 8, 9, 10)), rng.permutation(8)
    w[:, :, 8, 0, :, 9, 0] = 4
    for r in range(N):
        for j in range(8): w[r, :, 9, 0, o[(2 * r + j) % 8], 10, 0] = 512 if j < 4 else -512
    return {**d, "m": bonds(e), **weights(rng, w)}
def setup_inputs_near(rng):
    d = numbers_of(rng)
    x = d["x"].astype(np.float32).reshape(N, 8, 16, C, 4)
    x[:, :, :2] = 0
    x[:, :, 8:] = 0
    c = rng.choice([-1.0, 1.0], (N, 8, C))
    a = rng.choice([-1.0, 0.0, 1.0, 1.0], (3, N, 8, C))
    x[:, :, 0, :, 0] = c
    x[:, :, 1, :, 0] = -c
    x[:, :, 8, :, 0] = a[0] * 2.0 ** -30
    x[:, :, 9, :, 0] = a[1] * 2.0 ** -23
    x[:, :, 10, :, 0] = a[2] * 1.125 * 2.0 ** -30
    x[:, :, 11, :, 0] = a[2] * -1.0 * 2.0 ** -30
    u = d["u"].reshape(N, 128, 128, 4)
    u[:, :, ::16] = 0
    o = rng.permutation(N) % 3
    for r in range(N):
        if o[r] == 0:
            for g in rng.permutation(8)[:4]: x[r, g, 8, rng.integers(C), 0] = 2.0 ** 30 * rng.choice([-1.0, 1.0])
        for h in range(0, 128, 16):
            if o[r] == 0: u[r, h + 8, h, 0] = 2.0 ** -30
            elif o[r] == 1:
                u[r, h + 10, h, 0] = 1.125 * 2.0 ** -30
                u[r, h + 11, h, 0] = 1.25 * 2.0 ** -30
            else:
                for i in (0, 1, 9): u[r, h + i, h, 0] = 1
    return {"x": x.reshape(N, 128, 4 * C).astype(BF), "u": d["u"], "v": d["v"], "m": bonds(orders(rng)), **weights(rng, layers(rng, (0, 1, 8, 9, 10, 11, 12, 13, 14, 15)))}
def setup_inputs_late(rng):
    d = numbers_of(rng)
    k = np.argsort(rng.random((N, 8, C)), axis=1)
    known = k < 4 + (rng.permutation(N) % 2)[:, None, None]
    plant(d, np.where(k == 0, 0.0, np.where(known, 1.0, -1.0)))
    x = d["x"].reshape(N, 8, 16, C, 4)
    n = (N, 8, 8, C, 4)
    a = (1 + (2 * rng.integers(0, 64, n) + 1) * 2.0 ** -7) * np.exp2(rng.integers(-14, -7, n))
    a[:, :, 0, :, 0] = 1.96875
    x[:, :, 8:] = (a * (2.0 * rng.integers(0, 2, n) - 1.0)).astype(np.float32).astype(BF)
    x[:, :, 15, :, 0] = np.where(k == 0, faint(), 0.0).astype(np.float32).astype(BF)
    u = d["u"].reshape(N, 128, 128, 4)
    for h in range(0, 128, 16): u[:, h + 15, h, 0] = 1
    return {**d, "m": bonds(orders(rng)), **weights(rng, layers(rng))}
def setup_inputs_ends(rng):
    d = numbers_of(rng)
    x, e, c, i = np.zeros((N, 8, 16, C, 4)), orders(rng), int(rng.integers(4)), np.arange(128)
    u, v = d["u"].reshape(N, 128, 128, 4), d["v"]
    u[:, :, ::16] = 0
    w = np.zeros((N, 128, 4, 128, 4), np.float32)
    for r in range(N):
        k = (r + c) % 4
        a = (0.75 + 0.25 * rng.random((8, 16, C, 4))) * 2.0 ** 30
        for j in range(4): w[r, i, j, i, j] = 2.0 ** -30
        if k == 0:
            x[r] = a * rng.choice([-1.0, 1.0], C)[:, None]
            s = np.where(rng.permutation(8) < 5, 1.0, -1.0)
            for g in range(8): u[r, :, 16 * g] = s[g] * 2.0 ** 30
            e[r] = np.arange(C)[::-1]
            v[r] = (2.0 ** 30 * rng.choice([-1.0, 1.0], (128, 512))).astype(np.float32).astype(BF)
            n = i[i % 16 < 8]
            for j in range(4): w[r, n, j, n, j] = -1
        elif k == 1:
            x[r] = (1 + 0.25 * rng.integers(0, 4, (8, 16, C, 4))) * 2.0 ** -30
            x[r, :, :8] *= 2.0
            u[r, :, ::16] = 2.0 ** -30
            e[r] = np.arange(C)
            v[r] = (2.0 ** -30 * rng.choice([-1.0, 1.0], (128, 512))).astype(np.float32).astype(BF)
        elif k == 2:
            x[r] = -a
            u[r, :, ::16] = 2.0 ** 30
        else:
            x[r] = a * np.where(chosen(rng, H), 1.0, -1.0)[:, None, :, None]
            for g in range(8): u[r, 16 * g:16 * g + 16, 16 * g] = 2.0 ** 30
            e[r] = rng.permutation(C)
    return {"x": x.astype(np.float32).reshape(N, 128, 4 * C).astype(BF), "u": d["u"], "v": v, "m": bonds(e), **weights(rng, w.astype(BF))}
def setup_inputs_spread(rng):
    d = setup_inputs(rng)
    d["x"] = wide(rng, N, 128, 4 * C, cols=6)
    return d
def check_inputs(d):
    b = []
    for k in ("x", "u", "v"):
        a = np.abs(d[k].astype(np.float32))
        if not (np.isfinite(a).all() and ((a == 0) | (a >= 2.0 ** -30) & (a <= 2.0 ** 30)).all()): b.append("a value of " + k)
    none, least, most = [emit(mx_ref.quantize(np.full((128, 16), k, np.float32).astype(BF)))[1][0, 0] for k in (0.0, 2.0 ** -30, 2.0 ** 30)]
    for r in range(N):
        if (np.sort(gentries(d["m"][r]), axis=1) != np.arange(C)).any(): b.append("m: a list that is no permutation")
        if ((d["wc"][r] == 0x7F) | (d["wc"][r] == 0xFF)).any(): b.append("wc: a code that is no number")
        s = mx_ref.live(d["ws"][r])
        if ((s != none) & ((s < least) | (s > most))).any(): b.append("ws: a scale out of range")
    return b
def waves(s, to):
    w = np.where(s > 0, 1, 4)
    for t in (2, 3):
        licensed = np.count_nonzero(w < 4, axis=0) >= 5
        w = np.where((w == 4) & licensed[to], t, w)
    return w
def reference(x, u, v, m, wc, ws):
    qu = [mx_ref.quantize(u[r]) for r in range(N)]
    lay = [pk(wc[r], ws[r]) for r in range(N)]
    now = [x[r] for r in range(N)]
    lists = np.stack([gentries(m[r]) for r in range(N)])
    for t in range(R):
        to = np.roll(lists, -t, axis=1)
        own, wave, sent = [], [], []
        for r in range(N):
            q = mx_ref.quantize(now[r])
            own.append(decode(q).astype(BF))
            wave.append(waves(mx_ref.matmul(qu[r], q)[::16], to[r]))
            o = np.argsort(np.where(wave[r] < 4, 3 - wave[r], 3), axis=1, kind="stable")[:, :H]
            e = np.where(np.take_along_axis(wave[r], o, axis=1) < 4, o, -1)
            sent.append(mx_ref.quantize(gcols(own[r], e)))
        for r in range(N):
            guests = decode(sent[(r - 1) % N]).astype(BF)
            k = np.argsort(np.argsort(wave[r] < 4, axis=1, kind="stable"), axis=1)
            e = np.where(wave[r] == 1, np.arange(C), np.where(wave[r] < 4, to[r], C + k % H))
            z = gcols(np.concatenate([own[r], guests], axis=1), e)
            q = mx_ref.quantize(z)
            made = tile([mx_ref.matmul(pick(lay[r], np.arange(128 * b, 128 * b + 128)), q) * np.float32(0.03125) + z[:, b::4].astype(np.float32) for b in range(4)])
            now[r] = gcols(made, np.argsort(to[r], axis=1))
    y, wv = np.zeros((N, 128, C), np.float32), np.zeros((N, 8, C), np.float32)
    oc, osc = np.zeros((N, 128, 4 * C), np.uint8), np.zeros((N, 16, C), np.uint8)
    for r in range(N):
        q = mx_ref.quantize(now[r])
        y[r] = mx_ref.matmul(mx_ref.quantize(v[r]), q)
        wv[r] = wave[r]
        oc[r], osc[r] = emit(q)
    return {"y": y, "wv": wv, "oc": oc, "osc": osc}

@@ -1,0 +1,386 @@
+from concourse.mybir import dt, AluOpType, ActivationFunctionType
+
+HALF = "float16"
+R = 3
+BF, F32, I32, U16, U8, CODE = "bfloat16", "float32", "int32", "uint16", "uint8", "float8_e4m3fn_x4"
+
+SCRATCH = {"cst": ("sbuf", [128, 4096], BF), "sc": ("sbuf", [128, 3 * 392], HALF), "ho": ("sbuf", [128, 3 * 384], HALF),
+           "smi": ("sbuf", [128, 24 * 12], I32), "smf": ("sbuf", [128, 24 * 12], F32), "zo": ("sbuf", [128, 96], U16)}
+
+
+def _declare(names, width, dtype):
+    for n in names.split():
+        SCRATCH[n] = ("sbuf", [128, width], dtype)
+
+
+_declare("ones", 128, BF)
+_declare("ut vt", 512, BF)
+_declare("uq ur vq flq", 128, CODE)
+_declare("us urs vs fls", 128, U8)
+_declare("cq", 1024, CODE)
+_declare("cs", 1024, U8)
+_declare("wq", 512, CODE)
+_declare("wp", 512, U8)
+_declare("ui", 8, I32)
+_declare("uo", 8, U16)
+_declare("im16 im4 k16 r16 k4 r4 lic", 384, BF)
+_declare("m16 lk h4 ik ih", 384, HALF)
+_declare("fi gi inv yt wt", 384, F32)
+_declare("pI jI pw iw c2 bi", 24, I32)
+_declare("tc", 4, I32)
+_declare("tf nn", 4, F32)
+_declare("qu", 24, U16)
+_declare("z32 tt fp", 1536, BF)
+_declare("fl1 fl2 fl3", 528, BF)
+for _t in range(R):
+    _declare("mi%d dm%d" % (_t, _t), 24, I32)
+    _declare("mu%d iv%d ps%d pr%d" % (_t, _t, _t, _t), 24, U16)
+    _declare("fw%d" % _t, 3088, BF)
+    _declare("zt%d" % _t, 1536, BF)
+    _declare("aq%d gq%d zq%d" % (_t, _t, _t), 384, CODE)
+    _declare("as%d gs%d zs%d" % (_t, _t, _t), 384, U8)
+    _declare("wn%d" % _t, 1544, F32)
+for _t in range(R + 1):
+    _declare("xt%d" % _t, 1536, BF)
+    _declare("xq%d" % _t, 384, CODE)
+    _declare("xs%d" % _t, 384, U8)
+for _b in range(8):
+    SCRATCH["b%d" % _b] = ("psum", [128, 512], F32)
+
+SEMAPHORES = ["V", "S", "P", "G", "lx0", "lx1", "lu", "lv", "lw", "lm", "st", "rt"]
+for _t in range(R):
+    SEMAPHORES += ["aq%d" % _t, "lq%d" % _t, "ap%d" % _t, "lp%d" % _t]
+
+
+def rank_program(g, core, T, topo):
+    rank = T.rank_of(core)
+    if rank is None:
+        return
+    A, AF = AluOpType, ActivationFunctionType
+    cores = T.cores
+    nxt, prv = cores[(rank + 1) % len(cores)], cores[(rank - 1) % len(cores)]
+    qs = {"V": g.vector, "S": g.scalar, "P": g.tensor, "G": g, "Y": g.sync}
+    cnt, known, wr, rd = {}, {q: {} for q in qs}, {}, {}
+
+    def need(q, toks):
+        m = {}
+        for s, n in toks:
+            m[s] = max(n, m.get(s, 0))
+        for s in sorted(m):
+            if known[q].get(s, 0) < m[s]:
+                qs[q].wait_ge(T.sem[s], m[s])
+                known[q][s] = m[s]
+
+    def op(q, fn, reads, writes, sem=None, inc=1):
+        toks = []
+        for k in reads:
+            toks += wr.get(k, [])
+        for k in writes:
+            toks += wr.get(k, []) + rd.get(k, [])
+        need(q, toks)
+        s = sem or q
+        cnt[s] = cnt.get(s, 0) + inc
+        fn(qs[q]).then_inc(T.sem[s], inc)
+        for k in reads:
+            rd.setdefault(k, []).append((s, cnt[s]))
+        for k in writes:
+            wr[k], rd[k] = [(s, cnt[s])], []
+
+    def load(q, out, in_, sem):
+        cnt[sem] = cnt.get(sem, 0) + 16
+        qs[q].dma_start(out, in_).then_inc(T.sem[sem], 16)
+
+    def copy(out, in_, r, w):
+        op("V", lambda e: e.tensor_copy(out, in_), r, w)
+
+    def tt(out, a, b, o, r, w):
+        op("V", lambda e: e.tensor_tensor(out, a, b, o), r, w)
+
+    def ts(out, a, s1, o1, r, w, s2=None, o2=None):
+        if o2 is None:
+            op("V", lambda e: e.tensor_scalar(out, a, s1, None, o1), r, w)
+        else:
+            op("V", lambda e: e.tensor_scalar(out, a, s1, s2, o1, o2), r, w)
+
+    def fill(ap, c, w):
+        op("V", lambda e: e.memset(ap, c), [], w)
+
+    def scan(out, a, b, init, o1, o2, r, w):
+        op("V", lambda e: e.tensor_tensor_scan(out, a, b, init, o1, o2), r, w)
+
+    def quant(q, s, t, r, w):
+        op("V", lambda e: e.quantize_mx(q, s, t), r, w)
+
+    def mm(out, l, ls, m, ms, r, w):
+        op("P", lambda e: e.matmul_mx(out, l, ls, m, ms, True, True), r, w)
+
+    def act(out, in_, scale, r, w):
+        if scale is None:
+            op("S", lambda e: e.activation(out, in_, AF.Copy), r, w)
+        else:
+            op("S", lambda e: e.activation(out, in_, AF.Copy, scale=scale), r, w)
+
+    def iota(out, pat, base, cm, w):
+        op("G", lambda e: e.iota(out, pat, base, cm), [], w)
+
+    def iotaf(out, pat, base, cm, w):
+        op("G", lambda e: e.iota(out, pat, base, cm, allow_small_or_imprecise_dtypes=True), [], w)
+
+    def to_next(out, in_, rs, ls):
+        a = topo.addr(nxt)
+        cnt[ls] = cnt.get(ls, 0) + len(topo.engines(core, nxt))
+        g.remote_dma(out, in_, T.sem[rs], T.sem[ls], a[1], a[0], topo.mask(core, nxt))
+
+    arrive = len(topo.engines(prv, core))
+    smi = lambda j: T.smi[:, 24 * j:24 * j + 24]
+    smf = lambda j: T.smf[:, 24 * j:24 * j + 24]
+
+    load("S", T.ut[:], T.u[:], "lu")
+    load("Y", T.xt0[:, 0:768], T.x[:, 0:768], "lx0")
+    load("S", T.xt0[:, 768:1536], T.x[:, 768:1536], "lx1")
+    load("Y", T.mi0[:], T.m[:], "lm")
+    for t in range(1, R):
+        load("Y", T["mi%d" % t][0:128 - 16 * t, :], T.m[16 * t:128, :], "lm")
+        load("Y", T["mi%d" % t][128 - 16 * t:128, :], T.m[0:16 * t, :], "lm")
+    load("Y", T.wq[:].bitcast(dt.uint8), T.wc[:], "lw")
+    load("S", T.wp[:], T.ws[:], "lw")
+    load("S", T.vt[:], T.v[:], "lv")
+    wr["ut"], wr["x0a"], wr["x0b"] = [("lu", 16)], [("lx0", 16)], [("lx1", 16)]
+    wr["vt"], wr["W"] = [("lv", 16)], [("lw", 32)]
+    for t in range(R):
+        wr["mi%d" % t] = [("lm", cnt["lm"])]
+
+    iota(T.ui[:], [[16, 8]], 0, 0, ["ui"])
+    iota(T.pI[:], [[0, 24]], 0, 1, ["pI"])
+    iota(T.jI[:], [[16, 24]], 0, 0, ["jI"])
+    fill(T.ones[:], 1.0, ["ones"])
+    fill(T.cst[:, 0:2048], 0.0, ["cstE"])
+    fill(T.cst[:, 2048:4096], 0.0, ["cstC"])
+    for k in (2, 3):
+        act(T["fl%d" % k][:], T.cst[:, 2048:2576], None, ["cstC"], ["fl%d" % k])
+    for b in range(4):
+        op("G", lambda e, b=b: e.affine_select(T.cst[:, 512 * b + b:512 * b + 512:4], T.ones[:], [[-1, 128]], A.is_equal, 0.0, 0, 1),
+           ["ones", "cstE"], ["E%d" % b])
+    iotaf(T.im16[:], [[0, 24], [1, 16]], 0, 0, ["im16"])
+    fill(T.fl1[:], 0.0, ["fl1"])
+    copy(T.uo[:], T.ui[:], ["ui"], ["uo"])
+    ts(T.pw[:], T.pI[:], 15, A.bitwise_and, ["pI"], ["pw"])
+    copy(T.tf[:, 0:1], T.pw[:, 0:1], ["pw"], ["tf0"])
+    for b in range(4):
+        fill(T.cst[:, 2048 + 512 * b + b:2048 + 512 * b + 512:4], 1.0, ["C%d" % b, "cstC"])
+    quant(T.uq[:], T.us[:], T.ut[:], ["ut"], ["uq"])
+    copy(T.ur[:, 0:128].bitcast(dt.uint32), T.uq[:, 0:128].bitcast(dt.uint32).indirect(T.uo[:, 0:8]), ["uq", "uo"], ["ur"])
+    copy(T.urs[:, 0:128], T.us[:, 0:128].indirect(T.uo[:, 0:8]), ["uq", "uo"], ["urs"])
+
+    def late_constants_0():
+        quant(T.cq[:, 512:1024], T.cs[:, 512:1024], T.cst[:, 2048:4096], ["cstC", "C0", "C1", "C2", "C3"], ["cqC"])
+
+    def late_constants_1():
+        quant(T.cq[:, 0:512], T.cs[:, 0:512], T.cst[:, 0:2048], ["cstE", "E0", "E1", "E2", "E3"], ["cqE"])
+        ts(T.m16[:], T.im16[:], T.tf[:, 0:1], A.is_equal, ["im16", "tf0"], ["m16"], 4096.0, A.mult)
+        copy(T.mu0[:], T.mi0[:], ["mi0"], ["mu0"])
+
+    def late_constants_2():
+        tt(T.iw[:], T.pw[:], T.jI[:], A.add, ["pw", "jI"], ["iw"])
+        ts(T.bi[:], T.iw[:], 770.0, A.add, ["iw"], ["bi"])
+
+    def late_iotas_1():
+        iotaf(T.im4[:], [[0, 96], [1, 4]], 0, 0, ["im4"])
+        iotaf(T.fi[:], [[1, 384]], 0, 0, ["fi"])
+        iotaf(T.gi[:], [[1, 384]], 384, 0, ["gi"])
+
+    def late_iotas_2(t):
+        iotaf(T["wn%d" % t][:, 0:384], [[1, 384]], 0, 0, ["wna%d" % t])
+        iotaf(T["wn%d" % t][:, 384:648], [[0, 264]], 768, 0, ["wnb%d" % t])
+
+    def late_constants_3():
+        ts(T.c2[:], T.iw[:], 2.0, A.mult, ["iw"], ["c2"], 1.0, A.add)
+        ts(T.tc[:, 0:1], T.pw[:, 0:1], 12, A.bitwise_and, ["pw"], ["tc"])
+        ts(T.tc[:, 1:2], T.pw[:, 0:1], 3, A.bitwise_and, ["pw"], ["tc1"])
+        ts(T.tf[:, 1:2], T.tc[:, 0:1], 0.25, A.mult, ["tc"], ["tf1"])
+        copy(T.tf[:, 2:3], T.tc[:, 1:2], ["tc1"], ["tf"])
+        for t in range(R):
+            tt(T["dm%d" % t][:], T.iw[:], T["mi%d" % t][:], A.subtract, ["mi%d" % t, "iw"], ["dm%d" % t])
+            if t:
+                copy(T["mu%d" % t][:], T["mi%d" % t][:], ["mi%d" % t], ["mu%d" % t])
+            fill(T["fw%d" % t][:, 3072:3088], 0.0, ["fz%d" % t])
+        ts(T.k4[:], T.im4[:], T.tf[:, 1:2], A.is_equal, ["im4", "tf1"], ["k4"])
+        ts(T.r4[:], T.im4[:], 0.0, A.not_equal, ["im4"], ["r4"])
+
+    def inverse():
+        ts(T.k16[:], T.im16[:], T.tf[:, 0:1], A.is_equal, ["im16", "tf0"], ["k16"])
+        ts(T.r16[:], T.im16[:], 0.0, A.not_equal, ["im16"], ["r16"])
+        copy(T.inv[:, 0:384].indirect(T.mu0[:, 0:24]), T.fi[:], ["fi", "mu0"], ["inv"])
+        tt(T.ik[:], T.inv[:], T.k16[:], A.mult, ["inv", "k16"], ["ik"])
+        scan(T.ih[:], T.r16[:], T.ik[:], 0.0, A.mult, A.add, ["r16", "ik"], ["ih"])
+        copy(T.iv0[:], T.ih[:, 15:384:16], ["ih"], ["iv0"])
+        need("Y", wr["iv0"])
+        for t in range(1, R):
+            load("Y", T["iv%d" % t][0:128 - 16 * t, :], T.iv0[16 * t:128, :], "rt")
+            load("Y", T["iv%d" % t][128 - 16 * t:128, :], T.iv0[0:16 * t, :], "rt")
+        for t in range(1, R):
+            wr["iv%d" % t] = [("rt", cnt["rt"])]
+
+    E = lambda b: (T.cq[:, 128 * b:128 * b + 128], T.cs[:, 128 * b:128 * b + 128])
+    ONE = lambda b: (T.cq[:, 512 + 128 * b:640 + 128 * b], T.cs[:, 512 + 128 * b:640 + 128 * b])
+    bank = [T["b%d" % b] for b in range(8)]
+    hw = lambda k: T.ho[:, 384 * k - 369:384 * k:16]
+    N = lambda k: T.nn[:, k - 1:k]
+
+    def unpack(b, c, s, keys):
+        e, es = E(b)
+        mm(bank[b][:, 0:384], e, es, c, s, ["cqE"] + keys, ["B%d" % b])
+
+    def count(k):
+        quant(T.flq[:], T.fls[:], T["fl%d" % k][:, 16:528], ["fl%d" % k], ["flq"])
+        for b in range(4):
+            c, s = ONE(b)
+            mm(bank[4 + b][:, 0:128], c, s, T.flq[:], T.fls[:], ["cqC", "flq"], ["B%d" % (4 + b)])
+
+    def licence(k, t):
+        for b in range(4):
+            ts(T.lic[:, b:384:4], bank[4 + b][:, 0:96], 72.0, A.is_ge, ["B%d" % (4 + b)], ["lic%d" % b])
+        tt(T["fl%d" % (k + 1)][:, 16:400], T.lic[:, 0:384].indirect(T["mu%d" % t][:, 0:24]), T.fl1[:, 16:400], A.max,
+           ["lic0", "lic1", "lic2", "lic3", "mu%d" % t, "fl1"], ["fl%d" % (k + 1)])
+
+    def prefix(k):
+        f = T["fl%d" % k]
+        scan(T.sc[:, 392 * k - 392:392 * k - 6], f[:, 15:401], f[:, 16:402], float(k == 3), A.add, A.add, ["fl%d" % k], ["sc%d" % k])
+
+    def hold(k):
+        scan(T.ho[:, 384 * k - 384:384 * k], T.m16[:], T.sc[:, 392 * k - 392:392 * k - 8], 0.0, A.add, A.min, ["m16", "sc%d" % k], ["ho%d" % k])
+
+    for t in range(R):
+        x, xq, xs, u = T["xt%d" % t], T["xq%d" % t], T["xs%d" % t], t + 1
+        fw, gq, gs = T["fw%d" % t], T["gq%d" % t], T["gs%d" % t]
+        zt, zq, zs, wn = T["zt%d" % t], T["zq%d" % t], T["zs%d" % t], T["wn%d" % t]
+        XQ = ["xq%d0" % t, "xq%d1" % t]
+        for h in range(2):
+            src = ["x0" + "ab"[h]] if t == 0 else ["x%d%s" % (t, k) for k in "abcdef"]
+            c = slice(192 * h, 192 * h + 192)
+            quant(xq[:, c], xs[:, c], x[:, 768 * h:768 * h + 768], src, [XQ[h]])
+            mm(bank[4 + h][:, 0:192], T.ur[:], T.urs[:], xq[:, c], xs[:, c], ["ur", "urs", XQ[h]], ["B%d" % (4 + h)])
+        need("G", wr[XQ[1]])
+        to_next(T["aq%d" % t][:].bitcast(dt.uint8), xq[:].bitcast(dt.uint8), "aq%d" % t, "lq%d" % t)
+        to_next(T["as%d" % t][:], xs[:], "aq%d" % t, "lq%d" % t)
+        wr["aq%d" % t] = [("aq%d" % t, 2 * arrive)]
+        if t == 0:
+            late_iotas_1()
+            late_iotas_2(0)
+            late_constants_0()
+        for h in range(2):
+            ts(T.fl1[:, 16 + 192 * h:208 + 192 * h], bank[4 + h][:, 0:192], 0.0, A.is_gt, ["B%d" % (4 + h)], ["fl1"])
+        count(1)
+        if t == 0:
+            late_constants_1()
+        for b in range(2):
+            unpack(b, xq[:], xs[:], XQ)
+        prefix(1)
+        hold(1)
+        licence(1, t)
+        count(2)
+        for b in range(2, 4):
+            unpack(b, xq[:], xs[:], XQ)
+        for b in range(4):
+            act(fw[:, b:1536:4], bank[b][:, 0:384], None, ["B%d" % b], ["f%d%d" % (t, b)])
+        if t == 0:
+            late_constants_2()
+        prefix(2)
+        hold(2)
+        licence(2, t)
+        prefix(3)
+        copy(T.smi[:, 0:48], T.ho[:, 15:768:16], ["ho1", "ho2"], ["I12"])
+        copy(T.nn[:, 0:2], T.sc[:, 384:1168:392], ["sc1", "sc2"], ["n12"])
+        hold(3)
+        copy(N(3), T.sc[:, 1168:1169], ["sc3"], ["n3"])
+        ts(T.smi[:, 48:96], T.smi[:, 0:48], 1, A.bitwise_and, ["I12"], ["a12"])
+        copy(smi(4), hw(3), ["ho3"], ["I3"])
+        tt(smf(2), hw(2), hw(1), A.subtract, ["ho1", "ho2"], ["f2"])
+        ts(smf(0), hw(1), N(1), A.subtract, ["ho1", "n12", "n3"], ["f0"], N(3), A.add)
+        ts(smi(5), smi(4), 1, A.bitwise_and, ["I3"], ["na3"])
+        ts(smf(1), smf(2), N(2), A.subtract, ["f2", "n12", "n3"], ["f1"], N(3), A.add)
+        tt(smf(3), hw(3), hw(2), A.subtract, ["ho2", "ho3"], ["f3"])
+        tt(smf(7), smi(5), T.bi[:], A.mult, ["na3", "bi"], ["f7"])
+        tt(T.smf[:, 96:144], T.smf[:, 0:48], T.smi[:, 48:96], A.mult, ["f0", "f1", "a12"], ["f45"])
+        tt(smf(8), smf(3), smf(7), A.max, ["f3", "f7"], ["f8"])
+        tt(smf(9), smf(4), smf(5), A.max, ["f45"], ["f9"])
+        tt(smf(10), smf(8), smf(9), A.max, ["f8", "f9"], ["f10"])
+        copy(T["ps%d" % t][:], smf(10), ["f10"], ["ps%d" % t])
+        need("G", wr["ps%d" % t])
+        to_next(T["pr%d" % t][:], T["ps%d" % t][:], "ap%d" % t, "lp%d" % t)
+        wr["pr%d" % t] = [("ap%d" % t, arrive)]
+        if t == 0:
+            late_iotas_2(1)
+            late_iotas_2(2)
+
+        for b in range(4):
+            unpack(b, T["aq%d" % t][:], T["as%d" % t][:], ["aq%d" % t])
+            act(T.fp[:, b:1536:4], bank[b][:, 0:384], None, ["B%d" % b], ["p%d" % b])
+        if t == 0:
+            late_constants_3()
+        tt(smi(6), T.c2[:], smi(4), A.subtract, ["c2", "I3"], ["j6"])
+        tt(smi(7), smi(2), T["dm%d" % t][:], A.mult, ["a12", "dm%d" % t], ["j7"])
+        ts(smi(8), smi(6), 254, A.bitwise_and, ["j6"], ["j8"])
+        tt(smi(9), smi(7), T["mi%d" % t][:], A.add, ["j7", "mi%d" % t], ["j9"])
+        ts(smi(10), smi(8), 386.0, A.add, ["j8"], ["j10"])
+        tt(smi(6), smi(10), smi(5), A.mult, ["j10", "na3"], ["j6"])
+        tt(smi(11), smi(6), smi(9), A.max, ["j6", "j9"], ["j11"])
+        copy(T.qu[:], smi(11), ["j11"], ["qu"])
+        quant(gq[:], gs[:], T.fp[:], ["p0", "p1", "p2", "p3"], ["gq%d" % t])
+        for b in range(4):
+            unpack(b, gq[:], gs[:], ["gq%d" % t])
+            act(fw[:, 1536 + b:3072:4], bank[b][:, 0:384], None, ["B%d" % b], ["g%d%d" % (t, b)])
+        if t == 0:
+            inverse()
+
+        copy(wn[:, 384:1544].indirect(T["pr%d" % t][:, 0:24]), T.gi[:], ["gi", "pr%d" % t], ["wnb%d" % t])
+        tt(T.lk[:], wn[:, 0:648].indirect(T.qu[:, 0:24]), T.k4[:], A.mult, ["wna%d" % t, "wnb%d" % t, "qu", "k4"], ["lk"])
+        scan(T.h4[:], T.r4[:], T.lk[:], 0.0, A.mult, A.add, ["r4", "lk"], ["h4"])
+        ts(T.zo[:], T.h4[:, 3:384:4], 4.0, A.mult, ["h4", "tf"], ["zo"], T.tf[:, 2:3], A.add)
+        win = ["f%d%d" % (t, b) for b in range(4)] + ["g%d%d" % (t, b) for b in range(4)] + ["fz%d" % t, "zo"]
+        copy(zt[:, 0:768], fw[:, 0:3088].indirect(T.zo[:, 0:48]), win, ["za%d" % t])
+        act(zt[:, 768:1536], fw[:, 0:3088].indirect(T.zo[:, 48:96]), None, win, ["zb%d" % t])
+        Z = ["za%d" % t, "zb%d" % t]
+        quant(zq[:], zs[:], zt[:], Z, ["zq%d" % t])
+        ts(T.z32[:, 0:384], zt[:, 0:1536:4], 32.0, A.mult, Z, ["z0"])
+        for b in range(1, 4):
+            act(T.z32[:, 384 * b:384 * b + 384], zt[:, b:1536:4], 32.0, Z, ["z%d" % b])
+        for b in range(4):
+            mm(bank[b][:, 0:384], T.wq[:, 128 * b:128 * b + 128], T.wp[:, 128 * b:128 * b + 128], zq[:], zs[:], ["W", "zq%d" % t], ["B%d" % b])
+        if t == R - 1:
+            quant(T.vq[:], T.vs[:], T.vt[:], ["vt"], ["vq"])
+
+        xn, iv, ivk = T["xt%d" % u], T["iv%d" % t], ["iv%d" % t]
+        part = lambda b: T.tt[:, 384 * b:384 * b + 384]
+
+        def add(b):
+            tt(part(b), bank[b][:, 0:384], T.z32[:, 384 * b:384 * b + 384], A.add, ["B%d" % b, "z%d" % b], ["t%d" % b])
+        add(0)
+        add(1)
+        act(xn[:, 0:1536:4], part(0).indirect(iv[:, 0:24]), 0.03125, ["t0"] + ivk, ["x%da" % u])
+        act(xn[:, 1:1536:4], part(1).indirect(iv[:, 0:24]), 0.03125, ["t1"] + ivk, ["x%db" % u])
+        add(2)
+        add(3)
+        for b, k in ((2, "ce"), (3, "df")):
+            ts(xn[:, b:768:4], part(b).indirect(iv[:, 0:12]), 0.03125, A.mult, ["t%d" % b] + ivk, ["x%d%s" % (u, k[0])])
+            act(xn[:, 768 + b:1536:4], part(b).indirect(iv[:, 12:24]), 0.03125, ["t%d" % b] + ivk, ["x%d%s" % (u, k[1])])
+
+    x, xq, xs = T["xt%d" % R], T["xq%d" % R], T["xs%d" % R]
+    K2 = ["xq%d0" % R, "xq%d1" % R]
+    for h in range(2):
+        c = slice(192 * h, 192 * h + 192)
+        quant(xq[:, c], xs[:, c], x[:, 768 * h:768 * h + 768], ["x%d%s" % (R, s) for s in "abcdef"], [K2[h]])
+        mm(bank[4 + h][:, 0:192], T.vq[:], T.vs[:], xq[:, c], xs[:, c], ["vq", K2[h]], ["B%d" % (4 + h)])
+        if h == 0:
+            act(T.yt[:, c], bank[4][:, 0:192], None, ["B4"], ["y0"])
+    tt(T.wt[:], T.fl1[:, 16:400], T.fl2[:, 16:400], A.add, ["fl1", "fl2"], ["wt"])
+    copy(T.yt[:, 192:384], bank[5][:, 0:192], ["B5"], ["y1"])
+    tt(T.wt[:], T.wt[:], T.fl3[:, 16:400], A.add, ["wt", "fl3"], ["wt"])
+    ts(T.wt[:], T.wt[:], -1.0, A.mult, ["wt"], ["wt"], 4.0, A.add)
+    op("Y", lambda e: e.dma_start(T.oc[:], xq[:].bitcast(dt.uint8)), K2, [], "st", 16)
+    for k in range(4):
+        op("SY"[k % 2], lambda e, k=k: e.dma_start(T.osc[4 * k:4 * k + 4, :], xs[32 * k:32 * k + 4, :]), K2, [], "st", 16)
+    op("S", lambda e: e.dma_start(T.y[:, 0:192], T.yt[:, 0:192]), ["y0"], [], "st", 16)
+    op("S", lambda e: e.dma_start(T.y[:, 192:384], T.yt[:, 192:384]), ["y1"], [], "st", 16)
+    op("Y", lambda e: e.dma_start(T.wv[:], T.wt[0:128:16, :]), ["wt"], [], "st", 16)
+    need("G", [(s, n) for s, n in cnt.items()])

@@ -23,9 +23,9 @@ _declare("wq", 512, CODE)
 _declare("wp", 512, U8)
 _declare("ui", 8, I32)
 _declare("uo", 8, U16)
-_declare("im16 im4 k16 r16 k4 r4 lic", 384, BF)
-_declare("m16 lk h4 ik ih", 384, HALF)
-_declare("fi gi inv yt wt", 384, F32)
+_declare("im16 im4 m16 k16 r16 k4 r4 lic ab", 384, BF)
+_declare("lk h4 ik ih", 384, HALF)
+_declare("fi gi inv yt wt wx", 384, F32)
 _declare("pI jI pw iw c2 bi", 24, I32)
 _declare("tc", 4, I32)
 _declare("tf nn", 4, F32)
@@ -49,7 +49,7 @@ for _b in range(8):
 
 SEMAPHORES = ["V", "S", "P", "G", "lx0", "lx1", "lu", "lv", "lw", "lm", "st", "rt"]
 for _t in range(R):
-    SEMAPHORES += ["aq%d" % _t, "lq%d" % _t, "ap%d" % _t, "lp%d" % _t]
+    SEMAPHORES += ["aq%d" % _t, "ar%d" % _t, "lq%d" % _t, "ap%d" % _t, "lp%d" % _t]
 
 
 def rank_program(g, core, T, topo):
@@ -120,6 +120,9 @@ def rank_program(g, core, T, topo):
         else:
             op("S", lambda e: e.activation(out, in_, AF.Copy, scale=scale), r, w)
 
+    def fun(out, in_, f, r, w, bias=0.0, scale=1.0):
+        op("S", lambda e: e.activation(out, in_, f, bias=bias, scale=scale), r, w)
+
     def iota(out, pat, base, cm, w):
         op("G", lambda e: e.iota(out, pat, base, cm), [], w)
 
@@ -153,63 +156,70 @@ def rank_program(g, core, T, topo):
     iota(T.ui[:], [[16, 8]], 0, 0, ["ui"])
     iota(T.pI[:], [[0, 24]], 0, 1, ["pI"])
     iota(T.jI[:], [[16, 24]], 0, 0, ["jI"])
-    fill(T.ones[:], 1.0, ["ones"])
-    fill(T.cst[:, 0:2048], 0.0, ["cstE"])
-    fill(T.cst[:, 2048:4096], 0.0, ["cstC"])
-    for k in (2, 3):
-        act(T["fl%d" % k][:], T.cst[:, 2048:2576], None, ["cstC"], ["fl%d" % k])
-    for b in range(4):
-        op("G", lambda e, b=b: e.affine_select(T.cst[:, 512 * b + b:512 * b + 512:4], T.ones[:], [[-1, 128]], A.is_equal, 0.0, 0, 1),
-           ["ones", "cstE"], ["E%d" % b])
     iotaf(T.im16[:], [[0, 24], [1, 16]], 0, 0, ["im16"])
-    fill(T.fl1[:], 0.0, ["fl1"])
-    copy(T.uo[:], T.ui[:], ["ui"], ["uo"])
-    ts(T.pw[:], T.pI[:], 15, A.bitwise_and, ["pI"], ["pw"])
-    copy(T.tf[:, 0:1], T.pw[:, 0:1], ["pw"], ["tf0"])
+    fill(T.cst[:, 2048:4096], 0.0, ["cstC"])
     for b in range(4):
         fill(T.cst[:, 2048 + 512 * b + b:2048 + 512 * b + 512:4], 1.0, ["C%d" % b, "cstC"])
+    fun(T.cst[:, 0:1024], T.cst[:, 2048:3072], AF.Copy, ["cstC"], ["cstE0"], 0.0, 0.0)
+    iotaf(T.im4[:], [[0, 96], [1, 4]], 0, 0, ["im4"])
+    fill(T.ones[:], 1.0, ["ones"])
+    for c in (slice(0, 16), slice(400, 528)):
+        fill(T.fl1[:, c], 0.0, ["fl1"])
+    quant(T.cq[:, 512:1024], T.cs[:, 512:1024], T.cst[:, 2048:4096], ["cstC"], ["cqC"])
+    ts(T.pw[:], T.pI[:], 15, A.bitwise_and, ["pI"], ["pw"])
+    copy(T.uo[:], T.ui[:], ["ui"], ["uo"])
+    copy(T.tf[:, 0:1], T.pw[:, 0:1], ["pw"], ["tf0"])
+    ts(T.m16[:], T.im16[:], T.tf[:, 0:1], A.is_equal, ["im16", "tf0"], ["m16"], 4096.0, A.mult)
     quant(T.uq[:], T.us[:], T.ut[:], ["ut"], ["uq"])
     copy(T.ur[:, 0:128].bitcast(dt.uint32), T.uq[:, 0:128].bitcast(dt.uint32).indirect(T.uo[:, 0:8]), ["uq", "uo"], ["ur"])
-    copy(T.urs[:, 0:128], T.us[:, 0:128].indirect(T.uo[:, 0:8]), ["uq", "uo"], ["urs"])
+    act(T.urs[:, 0:128], T.us[:, 0:128].indirect(T.uo[:, 0:8]), None, ["uq", "uo"], ["urs"])
+    for k in (2, 3):
+        for c in (slice(0, 16), slice(400, 528)):
+            fun(T["fl%d" % k][:, c], T.fl1[:, c], AF.Copy, ["fl1"], ["fl%d" % k])
+    fun(T.cst[:, 1024:2048], T.cst[:, 2048:3072], AF.Copy, ["cstC"], ["cstE1"], 0.0, 0.0)
+    iotaf(T.fi[:], [[1, 384]], 0, 0, ["fi"])
 
-    def late_constants_0():
-        quant(T.cq[:, 512:1024], T.cs[:, 512:1024], T.cst[:, 2048:4096], ["cstC", "C0", "C1", "C2", "C3"], ["cqC"])
-
-    def late_constants_1():
-        quant(T.cq[:, 0:512], T.cs[:, 0:512], T.cst[:, 0:2048], ["cstE", "E0", "E1", "E2", "E3"], ["cqE"])
-        ts(T.m16[:], T.im16[:], T.tf[:, 0:1], A.is_equal, ["im16", "tf0"], ["m16"], 4096.0, A.mult)
-        copy(T.mu0[:], T.mi0[:], ["mi0"], ["mu0"])
-
-    def late_constants_2():
-        tt(T.iw[:], T.pw[:], T.jI[:], A.add, ["pw", "jI"], ["iw"])
-        ts(T.bi[:], T.iw[:], 770.0, A.add, ["iw"], ["bi"])
-
-    def late_iotas_1():
-        iotaf(T.im4[:], [[0, 96], [1, 4]], 0, 0, ["im4"])
-        iotaf(T.fi[:], [[1, 384]], 0, 0, ["fi"])
+    def late_calls_of_g():
+        for b in range(4):
+            op("G", lambda e, b=b: e.affine_select(T.cst[:, 512 * b + b:512 * b + 512:4], T.ones[:], [[-1, 128]], A.is_equal, 0.0, 0, 1),
+               ["ones", "cstE0", "cstE1"], ["E%d" % b])
         iotaf(T.gi[:], [[1, 384]], 384, 0, ["gi"])
 
-    def late_iotas_2(t):
+    def table(t):
         iotaf(T["wn%d" % t][:, 0:384], [[1, 384]], 0, 0, ["wna%d" % t])
         iotaf(T["wn%d" % t][:, 384:648], [[0, 264]], 768, 0, ["wnb%d" % t])
 
+    def late_constants_1():
+        fun(T.r16[:], T.im16[:], AF.Sign, ["im16"], ["r16"])
+        fun(T.r4[:], T.im4[:], AF.Sign, ["im4"], ["r4"])
+
+    def late_constants_2():
+        quant(T.cq[:, 0:512], T.cs[:, 0:512], T.cst[:, 0:2048], ["cstE0", "cstE1", "E0", "E1", "E2", "E3"], ["cqE"])
+        tt(T.iw[:], T.pw[:], T.jI[:], A.add, ["pw", "jI"], ["iw"])
+        ts(T.tc[:, 0:1], T.pw[:, 0:1], 12, A.bitwise_and, ["pw"], ["tc"])
+        ts(T.bi[:], T.iw[:], 770.0, A.add, ["iw"], ["bi"])
+        ts(T.tf[:, 1:2], T.tc[:, 0:1], 0.25, A.mult, ["tc"], ["tf1"])
+
+    def late_masks():
+        fun(T.ab[:], T.im16[:], AF.Abs, ["im16", "tf0"], ["ab"], T.tf[:, 0:1], -1.0)
+        fun(T.k16[:], T.ab[:], AF.Relu, ["ab"], ["k16"], 1.0, -1.0)
+        fun(T.ab[:], T.im4[:], AF.Abs, ["im4", "tf1"], ["ab"], T.tf[:, 1:2], -1.0)
+        fun(T.k4[:], T.ab[:], AF.Relu, ["ab"], ["k4"], 1.0, -1.0)
+
     def late_constants_3():
         ts(T.c2[:], T.iw[:], 2.0, A.mult, ["iw"], ["c2"], 1.0, A.add)
-        ts(T.tc[:, 0:1], T.pw[:, 0:1], 12, A.bitwise_and, ["pw"], ["tc"])
         ts(T.tc[:, 1:2], T.pw[:, 0:1], 3, A.bitwise_and, ["pw"], ["tc1"])
-        ts(T.tf[:, 1:2], T.tc[:, 0:1], 0.25, A.mult, ["tc"], ["tf1"])
+        tt(T.dm0[:], T.iw[:], T.mi0[:], A.subtract, ["mi0", "iw"], ["dm0"])
         copy(T.tf[:, 2:3], T.tc[:, 1:2], ["tc1"], ["tf"])
-        for t in range(R):
+        fill(T.fw0[:, 3072:3088], 0.0, ["fz0"])
+
+    def late_constants_4():
+        for t in range(1, R):
+            copy(T["mu%d" % t][:], T["mi%d" % t][:], ["mi%d" % t], ["mu%d" % t])
             tt(T["dm%d" % t][:], T.iw[:], T["mi%d" % t][:], A.subtract, ["mi%d" % t, "iw"], ["dm%d" % t])
-            if t:
-                copy(T["mu%d" % t][:], T["mi%d" % t][:], ["mi%d" % t], ["mu%d" % t])
             fill(T["fw%d" % t][:, 3072:3088], 0.0, ["fz%d" % t])
-        ts(T.k4[:], T.im4[:], T.tf[:, 1:2], A.is_equal, ["im4", "tf1"], ["k4"])
-        ts(T.r4[:], T.im4[:], 0.0, A.not_equal, ["im4"], ["r4"])
 
     def inverse():
-        ts(T.k16[:], T.im16[:], T.tf[:, 0:1], A.is_equal, ["im16", "tf0"], ["k16"])
-        ts(T.r16[:], T.im16[:], 0.0, A.not_equal, ["im16"], ["r16"])
         copy(T.inv[:, 0:384].indirect(T.mu0[:, 0:24]), T.fi[:], ["fi", "mu0"], ["inv"])
         tt(T.ik[:], T.inv[:], T.k16[:], A.mult, ["inv", "k16"], ["ik"])
         scan(T.ih[:], T.r16[:], T.ik[:], 0.0, A.mult, A.add, ["r16", "ik"], ["ih"])
@@ -227,9 +237,9 @@ def rank_program(g, core, T, topo):
     hw = lambda k: T.ho[:, 384 * k - 369:384 * k:16]
     N = lambda k: T.nn[:, k - 1:k]
 
-    def unpack(b, c, s, keys):
+    def unpack(b, k, c, s, w, keys):
         e, es = E(b)
-        mm(bank[b][:, 0:384], e, es, c, s, ["cqE"] + keys, ["B%d" % b])
+        mm(bank[k][:, 0:w], e, es, c, s, ["cqE"] + keys, ["B%d" % k])
 
     def count(k):
         quant(T.flq[:], T.fls[:], T["fl%d" % k][:, 16:528], ["fl%d" % k], ["flq"])
@@ -237,9 +247,13 @@ def rank_program(g, core, T, topo):
             c, s = ONE(b)
             mm(bank[4 + b][:, 0:128], c, s, T.flq[:], T.fls[:], ["cqC", "flq"], ["B%d" % (4 + b)])
 
-    def licence(k, t):
-        for b in range(4):
+    def licence(k, t, between):
+        for b in (0, 2):
+            fun(T.lic[:, b:384:4], bank[4 + b][:, 0:96], AF.Sign, ["B%d" % (4 + b)], ["lic%d" % b], -72.0)
+        for b in (1, 3):
             ts(T.lic[:, b:384:4], bank[4 + b][:, 0:96], 72.0, A.is_ge, ["B%d" % (4 + b)], ["lic%d" % b])
+            if b == 1:
+                between()
         tt(T["fl%d" % (k + 1)][:, 16:400], T.lic[:, 0:384].indirect(T["mu%d" % t][:, 0:24]), T.fl1[:, 16:400], A.max,
            ["lic0", "lic1", "lic2", "lic3", "mu%d" % t, "fl1"], ["fl%d" % (k + 1)])
 
@@ -250,72 +264,89 @@ def rank_program(g, core, T, topo):
     def hold(k):
         scan(T.ho[:, 384 * k - 384:384 * k], T.m16[:], T.sc[:, 392 * k - 392:392 * k - 8], 0.0, A.add, A.min, ["m16", "sc%d" % k], ["ho%d" % k])
 
+    def first_lists():
+        copy(T.smi[:, 0:48], T.ho[:, 15:768:16], ["ho1", "ho2"], ["I12"])
+        copy(T.nn[:, 0:2], T.sc[:, 384:1168:392], ["sc1", "sc2"], ["n12"])
+        tt(smf(2), hw(2), hw(1), A.subtract, ["ho1", "ho2"], ["f2"])
+
+    def first_bonds():
+        copy(T.mu0[:], T.mi0[:], ["mi0"], ["mu0"])
+
     for t in range(R):
         x, xq, xs, u = T["xt%d" % t], T["xq%d" % t], T["xs%d" % t], t + 1
         fw, gq, gs = T["fw%d" % t], T["gq%d" % t], T["gs%d" % t]
         zt, zq, zs, wn = T["zt%d" % t], T["zq%d" % t], T["zs%d" % t], T["wn%d" % t]
         XQ = ["xq%d0" % t, "xq%d1" % t]
         for h in range(2):
-            src = ["x0" + "ab"[h]] if t == 0 else ["x%d%s" % (t, k) for k in "abcdef"]
+            src = ["x0" + "ab"[h]] if t == 0 else ["x%d%s" % (t, k) for k in ("abcd", "abef")[h]]
             c = slice(192 * h, 192 * h + 192)
             quant(xq[:, c], xs[:, c], x[:, 768 * h:768 * h + 768], src, [XQ[h]])
             mm(bank[4 + h][:, 0:192], T.ur[:], T.urs[:], xq[:, c], xs[:, c], ["ur", "urs", XQ[h]], ["B%d" % (4 + h)])
         need("G", wr[XQ[1]])
-        to_next(T["aq%d" % t][:].bitcast(dt.uint8), xq[:].bitcast(dt.uint8), "aq%d" % t, "lq%d" % t)
-        to_next(T["as%d" % t][:], xs[:], "aq%d" % t, "lq%d" % t)
+        aq, sq = T["aq%d" % t], T["as%d" % t]
+        to_next(sq[:], xs[:], "aq%d" % t, "lq%d" % t)
+        to_next(aq[:, 0:192].bitcast(dt.uint8), xq[:, 0:192].bitcast(dt.uint8), "aq%d" % t, "lq%d" % t)
+        to_next(aq[:, 192:384].bitcast(dt.uint8), xq[:, 192:384].bitcast(dt.uint8), "ar%d" % t, "lq%d" % t)
         wr["aq%d" % t] = [("aq%d" % t, 2 * arrive)]
+        wr["ar%d" % t] = [("ar%d" % t, arrive)]
         if t == 0:
-            late_iotas_1()
-            late_iotas_2(0)
-            late_constants_0()
+            late_calls_of_g()
+            table(0)
         for h in range(2):
             ts(T.fl1[:, 16 + 192 * h:208 + 192 * h], bank[4 + h][:, 0:192], 0.0, A.is_gt, ["B%d" % (4 + h)], ["fl1"])
+
+        def own(b):
+            unpack(b, b, xq[:], xs[:], 384, XQ)
+            act(fw[:, b:1536:4], bank[b][:, 0:384], None, ["B%d" % b], ["f%d%d" % (t, b)])
         count(1)
-        if t == 0:
-            late_constants_1()
-        for b in range(2):
-            unpack(b, xq[:], xs[:], XQ)
         prefix(1)
         hold(1)
-        licence(1, t)
-        count(2)
-        for b in range(2, 4):
-            unpack(b, xq[:], xs[:], XQ)
-        for b in range(4):
-            act(fw[:, b:1536:4], bank[b][:, 0:384], None, ["B%d" % b], ["f%d%d" % (t, b)])
+        licence(1, t, first_bonds if t == 0 else lambda: None)
         if t == 0:
-            late_constants_2()
+            late_constants_1()
+        else:
+            own(0)
+            own(1)
+        count(2)
         prefix(2)
         hold(2)
-        licence(2, t)
+        if t == 0:
+            late_constants_2()
+        licence(2, t, first_lists)
+        if t == 0:
+            late_masks()
+            own(0)
+            own(1)
+        own(2)
+        own(3)
         prefix(3)
-        copy(T.smi[:, 0:48], T.ho[:, 15:768:16], ["ho1", "ho2"], ["I12"])
-        copy(T.nn[:, 0:2], T.sc[:, 384:1168:392], ["sc1", "sc2"], ["n12"])
+        ts(T.smi[:, 48:96], T.smi[:, 0:48], 1, A.bitwise_and, ["I12"], ["a12"])
         hold(3)
         copy(N(3), T.sc[:, 1168:1169], ["sc3"], ["n3"])
-        ts(T.smi[:, 48:96], T.smi[:, 0:48], 1, A.bitwise_and, ["I12"], ["a12"])
-        copy(smi(4), hw(3), ["ho3"], ["I3"])
-        tt(smf(2), hw(2), hw(1), A.subtract, ["ho1", "ho2"], ["f2"])
-        ts(smf(0), hw(1), N(1), A.subtract, ["ho1", "n12", "n3"], ["f0"], N(3), A.add)
-        ts(smi(5), smi(4), 1, A.bitwise_and, ["I3"], ["na3"])
-        ts(smf(1), smf(2), N(2), A.subtract, ["f2", "n12", "n3"], ["f1"], N(3), A.add)
         tt(smf(3), hw(3), hw(2), A.subtract, ["ho2", "ho3"], ["f3"])
-        tt(smf(7), smi(5), T.bi[:], A.mult, ["na3", "bi"], ["f7"])
+        copy(smi(4), hw(3), ["ho3"], ["I3"])
+        ts(smf(0), hw(1), N(1), A.subtract, ["ho1", "n12", "n3"], ["f0"], N(3), A.add)
+        ts(smf(1), smf(2), N(2), A.subtract, ["f2", "n12", "n3"], ["f1"], N(3), A.add)
+        ts(smi(5), smi(4), 1, A.bitwise_and, ["I3"], ["na3"])
         tt(T.smf[:, 96:144], T.smf[:, 0:48], T.smi[:, 48:96], A.mult, ["f0", "f1", "a12"], ["f45"])
-        tt(smf(8), smf(3), smf(7), A.max, ["f3", "f7"], ["f8"])
+        tt(smf(7), smi(5), T.bi[:], A.mult, ["na3", "bi"], ["f7"])
         tt(smf(9), smf(4), smf(5), A.max, ["f45"], ["f9"])
+        tt(smf(8), smf(3), smf(7), A.max, ["f3", "f7"], ["f8"])
         tt(smf(10), smf(8), smf(9), A.max, ["f8", "f9"], ["f10"])
         copy(T["ps%d" % t][:], smf(10), ["f10"], ["ps%d" % t])
         need("G", wr["ps%d" % t])
         to_next(T["pr%d" % t][:], T["ps%d" % t][:], "ap%d" % t, "lp%d" % t)
         wr["pr%d" % t] = [("ap%d" % t, arrive)]
         if t == 0:
-            late_iotas_2(1)
-            late_iotas_2(2)
+            table(1)
+            table(2)
 
-        for b in range(4):
-            unpack(b, T["aq%d" % t][:], T["as%d" % t][:], ["aq%d" % t])
-            act(T.fp[:, b:1536:4], bank[b][:, 0:384], None, ["B%d" % b], ["p%d" % b])
+        for h in range(2):
+            c = slice(192 * h, 192 * h + 192)
+            for b in range(4):
+                k = 4 * h + b
+                unpack(b, k, aq[:, c], sq[:, c], 192, ["aq%d" % t, "ar%d" % t][:h + 1])
+                act(T.fp[:, 768 * h + b:768 * h + 768:4], bank[k][:, 0:192], None, ["B%d" % k], ["p%d" % k])
         if t == 0:
             late_constants_3()
         tt(smi(6), T.c2[:], smi(4), A.subtract, ["c2", "I3"], ["j6"])
@@ -326,10 +357,15 @@ def rank_program(g, core, T, topo):
         tt(smi(6), smi(10), smi(5), A.mult, ["j10", "na3"], ["j6"])
         tt(smi(11), smi(6), smi(9), A.max, ["j6", "j9"], ["j11"])
         copy(T.qu[:], smi(11), ["j11"], ["qu"])
-        quant(gq[:], gs[:], T.fp[:], ["p0", "p1", "p2", "p3"], ["gq%d" % t])
-        for b in range(4):
-            unpack(b, gq[:], gs[:], ["gq%d" % t])
-            act(fw[:, 1536 + b:3072:4], bank[b][:, 0:384], None, ["B%d" % b], ["g%d%d" % (t, b)])
+        for h in range(2):
+            c = slice(192 * h, 192 * h + 192)
+            quant(gq[:, c], gs[:, c], T.fp[:, 768 * h:768 * h + 768], ["p%d" % k for k in range(4 * h, 4 * h + 4)], ["gq%d" % h])
+            for b in range(4):
+                k = 4 * h + b
+                unpack(b, k, gq[:, c], gs[:, c], 192, ["gq%d" % h])
+                act(fw[:, 1536 + 768 * h + b:2304 + 768 * h:4], bank[k][:, 0:192], None, ["B%d" % k], ["g%d" % k])
+        if t == R - 1:
+            tt(T.wt[:], T.fl1[:, 16:400], T.fl2[:, 16:400], A.add, ["fl1", "fl2"], ["wt"])
         if t == 0:
             inverse()
 
@@ -337,7 +373,7 @@ def rank_program(g, core, T, topo):
         tt(T.lk[:], wn[:, 0:648].indirect(T.qu[:, 0:24]), T.k4[:], A.mult, ["wna%d" % t, "wnb%d" % t, "qu", "k4"], ["lk"])
         scan(T.h4[:], T.r4[:], T.lk[:], 0.0, A.mult, A.add, ["r4", "lk"], ["h4"])
         ts(T.zo[:], T.h4[:, 3:384:4], 4.0, A.mult, ["h4", "tf"], ["zo"], T.tf[:, 2:3], A.add)
-        win = ["f%d%d" % (t, b) for b in range(4)] + ["g%d%d" % (t, b) for b in range(4)] + ["fz%d" % t, "zo"]
+        win = ["f%d%d" % (t, b) for b in range(4)] + ["g%d" % k for k in range(8)] + ["fz%d" % t, "zo"]
         copy(zt[:, 0:768], fw[:, 0:3088].indirect(T.zo[:, 0:48]), win, ["za%d" % t])
         act(zt[:, 768:1536], fw[:, 0:3088].indirect(T.zo[:, 48:96]), None, win, ["zb%d" % t])
         Z = ["za%d" % t, "zb%d" % t]
@@ -347,8 +383,11 @@ def rank_program(g, core, T, topo):
             act(T.z32[:, 384 * b:384 * b + 384], zt[:, b:1536:4], 32.0, Z, ["z%d" % b])
         for b in range(4):
             mm(bank[b][:, 0:384], T.wq[:, 128 * b:128 * b + 128], T.wp[:, 128 * b:128 * b + 128], zq[:], zs[:], ["W", "zq%d" % t], ["B%d" % b])
-        if t == R - 1:
+        if t == 0:
+            late_constants_4()
             quant(T.vq[:], T.vs[:], T.vt[:], ["vt"], ["vq"])
+        if t == R - 1:
+            tt(T.wx[:], T.wt[:], T.fl3[:, 16:400], A.add, ["wt", "fl3"], ["wx"])
 
         xn, iv, ivk = T["xt%d" % u], T["iv%d" % t], ["iv%d" % t]
         part = lambda b: T.tt[:, 384 * b:384 * b + 384]
@@ -369,17 +408,13 @@ def rank_program(g, core, T, topo):
     K2 = ["xq%d0" % R, "xq%d1" % R]
     for h in range(2):
         c = slice(192 * h, 192 * h + 192)
-        quant(xq[:, c], xs[:, c], x[:, 768 * h:768 * h + 768], ["x%d%s" % (R, s) for s in "abcdef"], [K2[h]])
+        quant(xq[:, c], xs[:, c], x[:, 768 * h:768 * h + 768], ["x%d%s" % (R, s) for s in ("abcd", "abef")[h]], [K2[h]])
         mm(bank[4 + h][:, 0:192], T.vq[:], T.vs[:], xq[:, c], xs[:, c], ["vq", K2[h]], ["B%d" % (4 + h)])
-        if h == 0:
-            act(T.yt[:, c], bank[4][:, 0:192], None, ["B4"], ["y0"])
-    tt(T.wt[:], T.fl1[:, 16:400], T.fl2[:, 16:400], A.add, ["fl1", "fl2"], ["wt"])
-    copy(T.yt[:, 192:384], bank[5][:, 0:192], ["B5"], ["y1"])
-    tt(T.wt[:], T.wt[:], T.fl3[:, 16:400], A.add, ["wt", "fl3"], ["wt"])
-    ts(T.wt[:], T.wt[:], -1.0, A.mult, ["wt"], ["wt"], 4.0, A.add)
+        act(T.yt[:, c], bank[4 + h][:, 0:192], None, ["B%d" % (4 + h)], ["y%d" % h])
+    ts(T.wt[:], T.wx[:], -1.0, A.mult, ["wx"], ["wt"], 4.0, A.add)
     op("Y", lambda e: e.dma_start(T.oc[:], xq[:].bitcast(dt.uint8)), K2, [], "st", 16)
     for k in range(4):
-        op("SY"[k % 2], lambda e, k=k: e.dma_start(T.osc[4 * k:4 * k + 4, :], xs[32 * k:32 * k + 4, :]), K2, [], "st", 16)
+        op("Y", lambda e, k=k: e.dma_start(T.osc[4 * k:4 * k + 4, :], xs[32 * k:32 * k + 4, :]), K2, [], "st", 16)
     op("S", lambda e: e.dma_start(T.y[:, 0:192], T.yt[:, 0:192]), ["y0"], [], "st", 16)
     op("S", lambda e: e.dma_start(T.y[:, 192:384], T.yt[:, 192:384]), ["y1"], [], "st", 16)
     op("Y", lambda e: e.dma_start(T.wv[:], T.wt[0:128:16, :]), ["wt"], [], "st", 16)

@@ -1,7 +1,8 @@
 from concourse.mybir import dt, AluOpType, ActivationFunctionType
 
 HALF = "float16"
-R = 3
+C, R = 384, 3
+CUT = 176
 BF, F32, I32, U16, U8, CODE = "bfloat16", "float32", "int32", "uint16", "uint8", "float8_e4m3fn_x4"
 
 SCRATCH = {"cst": ("sbuf", [128, 4096], BF), "sc": ("sbuf", [128, 3 * 392], HALF), "ho": ("sbuf", [128, 3 * 384], HALF),
@@ -26,7 +27,7 @@ _declare("uo", 8, U16)
 _declare("im16 im4 m16 k16 r16 k4 r4 lic ab", 384, BF)
 _declare("lk h4 ik ih", 384, HALF)
 _declare("fi gi inv yt wt wx", 384, F32)
-_declare("pI jI pw iw c2 bi", 24, I32)
+_declare("pI jI pw iw c2", 24, I32)
 _declare("tc", 4, I32)
 _declare("tf nn", 4, F32)
 _declare("qu", 24, U16)
@@ -90,6 +91,9 @@ def rank_program(g, core, T, topo):
         cnt[sem] = cnt.get(sem, 0) + 16
         qs[q].dma_start(out, in_).then_inc(T.sem[sem], 16)
 
+    def store(q, out, in_, r):
+        op(q, lambda e: e.dma_start(out, in_), r, [], "st", 16)
+
     def copy(out, in_, r, w):
         op("V", lambda e: e.tensor_copy(out, in_), r, w)
 
@@ -102,8 +106,8 @@ def rank_program(g, core, T, topo):
         else:
             op("V", lambda e: e.tensor_scalar(out, a, s1, s2, o1, o2), r, w)
 
-    def fill(ap, c, w):
-        op("V", lambda e: e.memset(ap, c), [], w)
+    def fill(ap, c, r, w):
+        op("V", lambda e: e.memset(ap, c), r, w)
 
     def scan(out, a, b, init, o1, o2, r, w):
         op("V", lambda e: e.tensor_tensor_scan(out, a, b, init, o1, o2), r, w)
@@ -145,10 +149,11 @@ def rank_program(g, core, T, topo):
     for t in range(1, R):
         load("Y", T["mi%d" % t][0:128 - 16 * t, :], T.m[16 * t:128, :], "lm")
         load("Y", T["mi%d" % t][128 - 16 * t:128, :], T.m[0:16 * t, :], "lm")
-    load("Y", T.wq[:].bitcast(dt.uint8), T.wc[:], "lw")
-    load("S", T.wp[:], T.ws[:], "lw")
-    load("S", T.vt[:], T.v[:], "lv")
     wr["ut"], wr["x0a"], wr["x0b"] = [("lu", 16)], [("lx0", 16)], [("lx1", 16)]
+    need("Y", wr["ut"] + wr["x0a"] + wr["x0b"])
+    load("Y", T.wq[:].bitcast(dt.uint8), T.wc[:], "lw")
+    load("Y", T.wp[:], T.ws[:], "lw")
+    load("Y", T.vt[:], T.v[:], "lv")
     wr["vt"], wr["W"] = [("lv", 16)], [("lw", 32)]
     for t in range(R):
         wr["mi%d" % t] = [("lm", cnt["lm"])]
@@ -157,26 +162,28 @@ def rank_program(g, core, T, topo):
     iota(T.pI[:], [[0, 24]], 0, 1, ["pI"])
     iota(T.jI[:], [[16, 24]], 0, 0, ["jI"])
     iotaf(T.im16[:], [[0, 24], [1, 16]], 0, 0, ["im16"])
-    fill(T.cst[:, 2048:4096], 0.0, ["cstC"])
+    fill(T.cst[:, 2048:4096], 0.0, [], ["cstC"])
     for b in range(4):
-        fill(T.cst[:, 2048 + 512 * b + b:2048 + 512 * b + 512:4], 1.0, ["C%d" % b, "cstC"])
-    fun(T.cst[:, 0:1024], T.cst[:, 2048:3072], AF.Copy, ["cstC"], ["cstE0"], 0.0, 0.0)
+        fill(T.cst[:, 2048 + 512 * b + b:2048 + 512 * b + 512:4], 1.0, ["cstC"], ["C%d" % b])
+    CC = ["cstC", "C0", "C1", "C2", "C3"]
+    fun(T.cst[:, 0:1024], T.cst[:, 2048:3072], AF.Copy, CC, ["cstE0"], 0.0, 0.0)
     iotaf(T.im4[:], [[0, 96], [1, 4]], 0, 0, ["im4"])
-    fill(T.ones[:], 1.0, ["ones"])
+    fill(T.ones[:], 1.0, [], ["ones"])
     for c in (slice(0, 16), slice(400, 528)):
-        fill(T.fl1[:, c], 0.0, ["fl1"])
-    quant(T.cq[:, 512:1024], T.cs[:, 512:1024], T.cst[:, 2048:4096], ["cstC"], ["cqC"])
+        fill(T.fl1[:, c], 0.0, [], ["fl1", "fl1z"])
+    quant(T.cq[:, 512:1024], T.cs[:, 512:1024], T.cst[:, 2048:4096], CC, ["cqC"])
     ts(T.pw[:], T.pI[:], 15, A.bitwise_and, ["pI"], ["pw"])
     copy(T.uo[:], T.ui[:], ["ui"], ["uo"])
     copy(T.tf[:, 0:1], T.pw[:, 0:1], ["pw"], ["tf0"])
-    ts(T.m16[:], T.im16[:], T.tf[:, 0:1], A.is_equal, ["im16", "tf0"], ["m16"], 4096.0, A.mult)
+    ts(T.tc[:, 0:1], T.pw[:, 0:1], 12, A.bitwise_and, ["pw"], ["tc"])
+    ts(T.tf[:, 1:2], T.tc[:, 0:1], 0.25, A.mult, ["tc"], ["tf1"])
     quant(T.uq[:], T.us[:], T.ut[:], ["ut"], ["uq"])
     copy(T.ur[:, 0:128].bitcast(dt.uint32), T.uq[:, 0:128].bitcast(dt.uint32).indirect(T.uo[:, 0:8]), ["uq", "uo"], ["ur"])
     act(T.urs[:, 0:128], T.us[:, 0:128].indirect(T.uo[:, 0:8]), None, ["uq", "uo"], ["urs"])
     for k in (2, 3):
         for c in (slice(0, 16), slice(400, 528)):
             fun(T["fl%d" % k][:, c], T.fl1[:, c], AF.Copy, ["fl1"], ["fl%d" % k])
-    fun(T.cst[:, 1024:2048], T.cst[:, 2048:3072], AF.Copy, ["cstC"], ["cstE1"], 0.0, 0.0)
+    fun(T.cst[:, 1024:2048], T.cst[:, 2048:3072], AF.Copy, CC, ["cstE1"], 0.0, 0.0)
     iotaf(T.fi[:], [[1, 384]], 0, 0, ["fi"])
 
     def late_calls_of_g():
@@ -192,13 +199,8 @@ def rank_program(g, core, T, topo):
     def late_constants_1():
         fun(T.r16[:], T.im16[:], AF.Sign, ["im16"], ["r16"])
         fun(T.r4[:], T.im4[:], AF.Sign, ["im4"], ["r4"])
-
-    def late_constants_2():
-        quant(T.cq[:, 0:512], T.cs[:, 0:512], T.cst[:, 0:2048], ["cstE0", "cstE1", "E0", "E1", "E2", "E3"], ["cqE"])
-        tt(T.iw[:], T.pw[:], T.jI[:], A.add, ["pw", "jI"], ["iw"])
-        ts(T.tc[:, 0:1], T.pw[:, 0:1], 12, A.bitwise_and, ["pw"], ["tc"])
-        ts(T.bi[:], T.iw[:], 770.0, A.add, ["iw"], ["bi"])
-        ts(T.tf[:, 1:2], T.tc[:, 0:1], 0.25, A.mult, ["tc"], ["tf1"])
+        for t in range(R):
+            fun(T["fw%d" % t][:, 3072:3088], T.fl1[:, 0:16], AF.Copy, ["fl1z"], ["fz%d" % t])
 
     def late_masks():
         fun(T.ab[:], T.im16[:], AF.Abs, ["im16", "tf0"], ["ab"], T.tf[:, 0:1], -1.0)
@@ -209,15 +211,7 @@ def rank_program(g, core, T, topo):
     def late_constants_3():
         ts(T.c2[:], T.iw[:], 2.0, A.mult, ["iw"], ["c2"], 1.0, A.add)
         ts(T.tc[:, 1:2], T.pw[:, 0:1], 3, A.bitwise_and, ["pw"], ["tc1"])
-        tt(T.dm0[:], T.iw[:], T.mi0[:], A.subtract, ["mi0", "iw"], ["dm0"])
         copy(T.tf[:, 2:3], T.tc[:, 1:2], ["tc1"], ["tf"])
-        fill(T.fw0[:, 3072:3088], 0.0, ["fz0"])
-
-    def late_constants_4():
-        for t in range(1, R):
-            copy(T["mu%d" % t][:], T["mi%d" % t][:], ["mi%d" % t], ["mu%d" % t])
-            tt(T["dm%d" % t][:], T.iw[:], T["mi%d" % t][:], A.subtract, ["mi%d" % t, "iw"], ["dm%d" % t])
-            fill(T["fw%d" % t][:, 3072:3088], 0.0, ["fz%d" % t])
 
     def inverse():
         copy(T.inv[:, 0:384].indirect(T.mu0[:, 0:24]), T.fi[:], ["fi", "mu0"], ["inv"])
@@ -267,10 +261,12 @@ def rank_program(g, core, T, topo):
     def first_lists():
         copy(T.smi[:, 0:48], T.ho[:, 15:768:16], ["ho1", "ho2"], ["I12"])
         copy(T.nn[:, 0:2], T.sc[:, 384:1168:392], ["sc1", "sc2"], ["n12"])
-        tt(smf(2), hw(2), hw(1), A.subtract, ["ho1", "ho2"], ["f2"])
+        tt(smf(0), hw(2), hw(1), A.subtract, ["ho1", "ho2"], ["f2"])
 
     def first_bonds():
+        tt(T.iw[:], T.pw[:], T.jI[:], A.add, ["pw", "jI"], ["iw"])
         copy(T.mu0[:], T.mi0[:], ["mi0"], ["mu0"])
+        ts(smf(8), T.iw[:], 770.0, A.add, ["iw"], ["bi"])
 
     for t in range(R):
         x, xq, xs, u = T["xt%d" % t], T["xq%d" % t], T["xs%d" % t], t + 1
@@ -292,6 +288,7 @@ def rank_program(g, core, T, topo):
         if t == 0:
             late_calls_of_g()
             table(0)
+            ts(T.m16[:], T.im16[:], T.tf[:, 0:1], A.is_equal, ["im16", "tf0"], ["m16"], 4096.0, A.mult)
         for h in range(2):
             ts(T.fl1[:, 16 + 192 * h:208 + 192 * h], bank[4 + h][:, 0:192], 0.0, A.is_gt, ["B%d" % (4 + h)], ["fl1"])
 
@@ -311,29 +308,30 @@ def rank_program(g, core, T, topo):
         prefix(2)
         hold(2)
         if t == 0:
-            late_constants_2()
+            quant(T.cq[:, 0:512], T.cs[:, 0:512], T.cst[:, 0:2048], ["cstE0", "cstE1", "E0", "E1", "E2", "E3"], ["cqE"])
         licence(2, t, first_lists)
         if t == 0:
             late_masks()
             own(0)
             own(1)
-        own(2)
-        own(3)
+        else:
+            own(2)
+            own(3)
+        if t == R - 1:
+            fun(T.wt[:], T.fl1[:, 16:400], AF.Copy, ["fl1"], ["wt"], 4.0, -1.0)
         prefix(3)
         ts(T.smi[:, 48:96], T.smi[:, 0:48], 1, A.bitwise_and, ["I12"], ["a12"])
         hold(3)
         copy(N(3), T.sc[:, 1168:1169], ["sc3"], ["n3"])
-        tt(smf(3), hw(3), hw(2), A.subtract, ["ho2", "ho3"], ["f3"])
-        copy(smi(4), hw(3), ["ho3"], ["I3"])
-        ts(smf(0), hw(1), N(1), A.subtract, ["ho1", "n12", "n3"], ["f0"], N(3), A.add)
-        ts(smf(1), smf(2), N(2), A.subtract, ["f2", "n12", "n3"], ["f1"], N(3), A.add)
-        ts(smi(5), smi(4), 1, A.bitwise_and, ["I3"], ["na3"])
-        tt(T.smf[:, 96:144], T.smf[:, 0:48], T.smi[:, 48:96], A.mult, ["f0", "f1", "a12"], ["f45"])
-        tt(smf(7), smi(5), T.bi[:], A.mult, ["na3", "bi"], ["f7"])
-        tt(smf(9), smf(4), smf(5), A.max, ["f45"], ["f9"])
-        tt(smf(8), smf(3), smf(7), A.max, ["f3", "f7"], ["f8"])
-        tt(smf(10), smf(8), smf(9), A.max, ["f8", "f9"], ["f10"])
-        copy(T["ps%d" % t][:], smf(10), ["f10"], ["ps%d" % t])
+        copy(smi(5), hw(3), ["ho3"], ["I3"])
+        tt(smf(4), hw(3), hw(2), A.subtract, ["ho2", "ho3"], ["f4"])
+        ts(smf(6), hw(1), N(1), A.subtract, ["ho1", "n12", "n3"], ["f6"], N(3), A.add)
+        ts(smi(4), smi(5), 1, A.bitwise_and, ["I3"], ["na3"])
+        ts(smf(7), smf(0), N(2), A.subtract, ["f2", "n12", "n3"], ["f7"], N(3), A.add)
+        tt(T.smf[:, 24:96], T.smf[:, 144:216], T.smi[:, 48:120], A.mult, ["f6", "f7", "bi", "a12", "na3"], ["f123"])
+        tt(T.smf[:, 216:264], T.smf[:, 24:72], T.smf[:, 72:120], A.max, ["f123", "f4"], ["f9"])
+        tt(smf(5), smf(9), smf(10), A.max, ["f9"], ["f5"])
+        copy(T["ps%d" % t][:], smf(5), ["f5"], ["ps%d" % t])
         need("G", wr["ps%d" % t])
         to_next(T["pr%d" % t][:], T["ps%d" % t][:], "ap%d" % t, "lp%d" % t)
         wr["pr%d" % t] = [("ap%d" % t, arrive)]
@@ -348,15 +346,21 @@ def rank_program(g, core, T, topo):
                 unpack(b, k, aq[:, c], sq[:, c], 192, ["aq%d" % t, "ar%d" % t][:h + 1])
                 act(T.fp[:, 768 * h + b:768 * h + 768:4], bank[k][:, 0:192], None, ["B%d" % k], ["p%d" % k])
         if t == 0:
+            own(2)
+            own(3)
+        if t == 0:
             late_constants_3()
-        tt(smi(6), T.c2[:], smi(4), A.subtract, ["c2", "I3"], ["j6"])
-        tt(smi(7), smi(2), T["dm%d" % t][:], A.mult, ["a12", "dm%d" % t], ["j7"])
+        tt(smi(6), T.c2[:], smi(5), A.subtract, ["c2", "I3"], ["j6"])
+        tt(T["dm%d" % t][:], T.iw[:], T["mi%d" % t][:], A.subtract, ["mi%d" % t, "iw"], ["dm%d" % t])
         ts(smi(8), smi(6), 254, A.bitwise_and, ["j6"], ["j8"])
-        tt(smi(9), smi(7), T["mi%d" % t][:], A.add, ["j7", "mi%d" % t], ["j9"])
+        tt(smi(7), smi(2), T["dm%d" % t][:], A.mult, ["a12", "dm%d" % t], ["j7"])
         ts(smi(10), smi(8), 386.0, A.add, ["j8"], ["j10"])
-        tt(smi(6), smi(10), smi(5), A.mult, ["j10", "na3"], ["j6"])
+        tt(smi(9), smi(7), T["mi%d" % t][:], A.add, ["j7", "mi%d" % t], ["j9"])
+        tt(smi(6), smi(10), smi(4), A.mult, ["j10", "na3"], ["j6"])
         tt(smi(11), smi(6), smi(9), A.max, ["j6", "j9"], ["j11"])
         copy(T.qu[:], smi(11), ["j11"], ["qu"])
+        if t == R - 1:
+            tt(T.wt[:], T.wt[:], T.fl2[:, 16:400], A.subtract, ["fl2", "wt"], ["wt"])
         for h in range(2):
             c = slice(192 * h, 192 * h + 192)
             quant(gq[:, c], gs[:, c], T.fp[:, 768 * h:768 * h + 768], ["p%d" % k for k in range(4 * h, 4 * h + 4)], ["gq%d" % h])
@@ -364,46 +368,59 @@ def rank_program(g, core, T, topo):
                 k = 4 * h + b
                 unpack(b, k, gq[:, c], gs[:, c], 192, ["gq%d" % h])
                 act(fw[:, 1536 + 768 * h + b:2304 + 768 * h:4], bank[k][:, 0:192], None, ["B%d" % k], ["g%d" % k])
-        if t == R - 1:
-            tt(T.wt[:], T.fl1[:, 16:400], T.fl2[:, 16:400], A.add, ["fl1", "fl2"], ["wt"])
-        if t == 0:
-            inverse()
+        if u < R:
+            copy(T["mu%d" % u][:], T["mi%d" % u][:], ["mi%d" % u], ["mu%d" % u])
+        if t == 1:
+            quant(T.vq[:], T.vs[:], T.vt[:], ["vt"], ["vq"])
 
         copy(wn[:, 384:1544].indirect(T["pr%d" % t][:, 0:24]), T.gi[:], ["gi", "pr%d" % t], ["wnb%d" % t])
         tt(T.lk[:], wn[:, 0:648].indirect(T.qu[:, 0:24]), T.k4[:], A.mult, ["wna%d" % t, "wnb%d" % t, "qu", "k4"], ["lk"])
         scan(T.h4[:], T.r4[:], T.lk[:], 0.0, A.mult, A.add, ["r4", "lk"], ["h4"])
         ts(T.zo[:], T.h4[:, 3:384:4], 4.0, A.mult, ["h4", "tf"], ["zo"], T.tf[:, 2:3], A.add)
         win = ["f%d%d" % (t, b) for b in range(4)] + ["g%d" % k for k in range(8)] + ["fz%d" % t, "zo"]
-        copy(zt[:, 0:768], fw[:, 0:3088].indirect(T.zo[:, 0:48]), win, ["za%d" % t])
-        act(zt[:, 768:1536], fw[:, 0:3088].indirect(T.zo[:, 48:96]), None, win, ["zb%d" % t])
+        P2 = (slice(0, CUT), slice(CUT, C))
+        wide = (CUT, C - CUT)
         Z = ["za%d" % t, "zb%d" % t]
-        quant(zq[:], zs[:], zt[:], Z, ["zq%d" % t])
-        ts(T.z32[:, 0:384], zt[:, 0:1536:4], 32.0, A.mult, Z, ["z0"])
-        for b in range(1, 4):
-            act(T.z32[:, 384 * b:384 * b + 384], zt[:, b:1536:4], 32.0, Z, ["z%d" % b])
-        for b in range(4):
-            mm(bank[b][:, 0:384], T.wq[:, 128 * b:128 * b + 128], T.wp[:, 128 * b:128 * b + 128], zq[:], zs[:], ["W", "zq%d" % t], ["B%d" % b])
+        for h in (0, 1):
+            f4, off = slice(4 * P2[h].start, 4 * P2[h].stop), T.zo[:, P2[h].start // 4:P2[h].stop // 4]
+            if h == 0 and t > 0:
+                copy(zt[:, f4], fw[:, 0:3088].indirect(off), win, [Z[h]])
+            else:
+                act(zt[:, f4], fw[:, 0:3088].indirect(off), None, win, [Z[h]])
         if t == 0:
-            late_constants_4()
-            quant(T.vq[:], T.vs[:], T.vt[:], ["vt"], ["vq"])
+            inverse()
+        for h in (0, 1):
+            quant(zq[:, P2[h]], zs[:, P2[h]], zt[:, 4 * P2[h].start:4 * P2[h].stop], [Z[h]], ["zq%d" % h])
+        ts(T.z32[:, 0:C], zt[:, 0:4 * C:4], 32.0, A.mult, Z, ["z0"])
+        for b in range(1, 4):
+            act(T.z32[:, C * b:C * b + C], zt[:, b:4 * C:4], 32.0, Z, ["z%d" % b])
+        for b in range(4):
+            for h in (0, 1):
+                k = 4 * h + b
+                mm(bank[k][:, 0:wide[h]], T.wq[:, 128 * b:128 * b + 128], T.wp[:, 128 * b:128 * b + 128],
+                   zq[:, P2[h]], zs[:, P2[h]], ["W", "zq%d" % h], ["B%d" % k])
         if t == R - 1:
-            tt(T.wx[:], T.wt[:], T.fl3[:, 16:400], A.add, ["wt", "fl3"], ["wx"])
+            tt(T.wx[:], T.wt[:], T.fl3[:, 16:400], A.subtract, ["wt", "fl3"], ["wx"])
 
         xn, iv, ivk = T["xt%d" % u], T["iv%d" % t], ["iv%d" % t]
-        part = lambda b: T.tt[:, 384 * b:384 * b + 384]
+        part = lambda b: T.tt[:, C * b:C * b + C]
 
         def add(b):
-            tt(part(b), bank[b][:, 0:384], T.z32[:, 384 * b:384 * b + 384], A.add, ["B%d" % b, "z%d" % b], ["t%d" % b])
+            for h in (0, 1):
+                c, k = slice(C * b + P2[h].start, C * b + P2[h].stop), 4 * h + b
+                tt(T.tt[:, c], bank[k][:, 0:wide[h]], T.z32[:, c], A.add, ["B%d" % k, "z%d" % b], ["t%d%d" % (b, h)])
         add(0)
         add(1)
-        act(xn[:, 0:1536:4], part(0).indirect(iv[:, 0:24]), 0.03125, ["t0"] + ivk, ["x%da" % u])
-        act(xn[:, 1:1536:4], part(1).indirect(iv[:, 0:24]), 0.03125, ["t1"] + ivk, ["x%db" % u])
+        act(xn[:, 0:1536:4], part(0).indirect(iv[:, 0:24]), 0.03125, ["t00", "t01"] + ivk, ["x%da" % u])
+        act(xn[:, 1:1536:4], part(1).indirect(iv[:, 0:24]), 0.03125, ["t10", "t11"] + ivk, ["x%db" % u])
         add(2)
         add(3)
         for b, k in ((2, "ce"), (3, "df")):
-            ts(xn[:, b:768:4], part(b).indirect(iv[:, 0:12]), 0.03125, A.mult, ["t%d" % b] + ivk, ["x%d%s" % (u, k[0])])
-            act(xn[:, 768 + b:1536:4], part(b).indirect(iv[:, 12:24]), 0.03125, ["t%d" % b] + ivk, ["x%d%s" % (u, k[1])])
+            tk = ["t%d0" % b, "t%d1" % b] + ivk
+            ts(xn[:, b:768:4], part(b).indirect(iv[:, 0:12]), 0.03125, A.mult, tk, ["x%d%s" % (u, k[0])])
+            act(xn[:, 768 + b:1536:4], part(b).indirect(iv[:, 12:24]), 0.03125, tk, ["x%d%s" % (u, k[1])])
 
+    store("Y", T.wv[:], T.wx[0:128:16, :], ["wx"])
     x, xq, xs = T["xt%d" % R], T["xq%d" % R], T["xs%d" % R]
     K2 = ["xq%d0" % R, "xq%d1" % R]
     for h in range(2):
@@ -411,11 +428,9 @@ def rank_program(g, core, T, topo):
         quant(xq[:, c], xs[:, c], x[:, 768 * h:768 * h + 768], ["x%d%s" % (R, s) for s in ("abcd", "abef")[h]], [K2[h]])
         mm(bank[4 + h][:, 0:192], T.vq[:], T.vs[:], xq[:, c], xs[:, c], ["vq", K2[h]], ["B%d" % (4 + h)])
         act(T.yt[:, c], bank[4 + h][:, 0:192], None, ["B%d" % (4 + h)], ["y%d" % h])
-    ts(T.wt[:], T.wx[:], -1.0, A.mult, ["wx"], ["wt"], 4.0, A.add)
-    op("Y", lambda e: e.dma_start(T.oc[:], xq[:].bitcast(dt.uint8)), K2, [], "st", 16)
+        store("Y", T.oc[:, 768 * h:768 * h + 768], xq[:, c].bitcast(dt.uint8), [K2[h]])
+    store("S", T.y[:, 192:384], T.yt[:, 192:384], ["y1"])
+    store("Y", T.y[:, 0:192], T.yt[:, 0:192], ["y0"])
     for k in range(4):
-        op("Y", lambda e, k=k: e.dma_start(T.osc[4 * k:4 * k + 4, :], xs[32 * k:32 * k + 4, :]), K2, [], "st", 16)
-    op("S", lambda e: e.dma_start(T.y[:, 0:192], T.yt[:, 0:192]), ["y0"], [], "st", 16)
-    op("S", lambda e: e.dma_start(T.y[:, 192:384], T.yt[:, 192:384]), ["y1"], [], "st", 16)
-    op("Y", lambda e: e.dma_start(T.wv[:], T.wt[0:128:16, :]), ["wt"], [], "st", 16)
+        store("YS"[k % 2], T.osc[4 * k:4 * k + 4, :], xs[32 * k:32 * k + 4, :], K2)
     need("G", [(s, n) for s, n in cnt.items()])

from concourse.mybir import dt, AluOpType, ActivationFunctionType

HALF = "float16"
C, R = 384, 3
CUT = 176
BF, F32, I32, U16, U8, CODE = "bfloat16", "float32", "int32", "uint16", "uint8", "float8_e4m3fn_x4"

SCRATCH = {"cst": ("sbuf", [128, 4096], BF), "sc": ("sbuf", [128, 3 * 392], HALF), "ho": ("sbuf", [128, 3 * 384], HALF),
           "smi": ("sbuf", [128, 24 * 12], I32), "smf": ("sbuf", [128, 24 * 12], F32), "zo": ("sbuf", [128, 96], U16)}


def _declare(names, width, dtype):
    for n in names.split():
        SCRATCH[n] = ("sbuf", [128, width], dtype)


_declare("ones", 128, BF)
_declare("ut vt", 512, BF)
_declare("uq ur vq flq", 128, CODE)
_declare("us urs vs fls", 128, U8)
_declare("cq", 1024, CODE)
_declare("cs", 1024, U8)
_declare("wq", 512, CODE)
_declare("wp", 512, U8)
_declare("ui", 8, I32)
_declare("uo", 8, U16)
_declare("im16 im4 m16 k16 r16 k4 r4 lic ab", 384, BF)
_declare("lk h4 ik ih", 384, HALF)
_declare("fi gi inv yt wt wx", 384, F32)
_declare("pI jI pw iw c2", 24, I32)
_declare("tc", 4, I32)
_declare("tf nn", 4, F32)
_declare("qu", 24, U16)
_declare("z32 tt fp", 1536, BF)
_declare("fl1 fl2 fl3", 528, BF)
for _t in range(R):
    _declare("mi%d dm%d" % (_t, _t), 24, I32)
    _declare("mu%d iv%d ps%d pr%d" % (_t, _t, _t, _t), 24, U16)
    _declare("fw%d" % _t, 3088, BF)
    _declare("zt%d" % _t, 1536, BF)
    _declare("aq%d gq%d zq%d" % (_t, _t, _t), 384, CODE)
    _declare("as%d gs%d zs%d" % (_t, _t, _t), 384, U8)
    _declare("wn%d" % _t, 1544, F32)
for _t in range(R + 1):
    _declare("xt%d" % _t, 1536, BF)
    _declare("xq%d" % _t, 384, CODE)
    _declare("xs%d" % _t, 384, U8)
for _b in range(8):
    SCRATCH["b%d" % _b] = ("psum", [128, 512], F32)

SEMAPHORES = ["V", "S", "P", "G", "lx0", "lx1", "lu", "lv", "lw", "lm", "st", "rt"]
for _t in range(R):
    SEMAPHORES += ["aq%d" % _t, "ar%d" % _t, "lq%d" % _t, "ap%d" % _t, "lp%d" % _t]


def rank_program(g, core, T, topo):
    rank = T.rank_of(core)
    if rank is None:
        return
    A, AF = AluOpType, ActivationFunctionType
    cores = T.cores
    nxt, prv = cores[(rank + 1) % len(cores)], cores[(rank - 1) % len(cores)]
    qs = {"V": g.vector, "S": g.scalar, "P": g.tensor, "G": g, "Y": g.sync}
    cnt, known, wr, rd = {}, {q: {} for q in qs}, {}, {}

    def need(q, toks):
        m = {}
        for s, n in toks:
            m[s] = max(n, m.get(s, 0))
        for s in sorted(m):
            if known[q].get(s, 0) < m[s]:
                qs[q].wait_ge(T.sem[s], m[s])
                known[q][s] = m[s]

    def op(q, fn, reads, writes, sem=None, inc=1):
        toks = []
        for k in reads:
            toks += wr.get(k, [])
        for k in writes:
            toks += wr.get(k, []) + rd.get(k, [])
        need(q, toks)
        s = sem or q
        cnt[s] = cnt.get(s, 0) + inc
        fn(qs[q]).then_inc(T.sem[s], inc)
        for k in reads:
            rd.setdefault(k, []).append((s, cnt[s]))
        for k in writes:
            wr[k], rd[k] = [(s, cnt[s])], []

    def load(q, out, in_, sem):
        cnt[sem] = cnt.get(sem, 0) + 16
        qs[q].dma_start(out, in_).then_inc(T.sem[sem], 16)

    def store(q, out, in_, r):
        op(q, lambda e: e.dma_start(out, in_), r, [], "st", 16)

    def copy(out, in_, r, w):
        op("V", lambda e: e.tensor_copy(out, in_), r, w)

    def tt(out, a, b, o, r, w):
        op("V", lambda e: e.tensor_tensor(out, a, b, o), r, w)

    def ts(out, a, s1, o1, r, w, s2=None, o2=None):
        if o2 is None:
            op("V", lambda e: e.tensor_scalar(out, a, s1, None, o1), r, w)
        else:
            op("V", lambda e: e.tensor_scalar(out, a, s1, s2, o1, o2), r, w)

    def fill(ap, c, r, w):
        op("V", lambda e: e.memset(ap, c), r, w)

    def scan(out, a, b, init, o1, o2, r, w):
        op("V", lambda e: e.tensor_tensor_scan(out, a, b, init, o1, o2), r, w)

    def quant(q, s, t, r, w):
        op("V", lambda e: e.quantize_mx(q, s, t), r, w)

    def mm(out, l, ls, m, ms, r, w):
        op("P", lambda e: e.matmul_mx(out, l, ls, m, ms, True, True), r, w)

    def act(out, in_, scale, r, w):
        if scale is None:
            op("S", lambda e: e.activation(out, in_, AF.Copy), r, w)
        else:
            op("S", lambda e: e.activation(out, in_, AF.Copy, scale=scale), r, w)

    def fun(out, in_, f, r, w, bias=0.0, scale=1.0):
        op("S", lambda e: e.activation(out, in_, f, bias=bias, scale=scale), r, w)

    def iota(out, pat, base, cm, w):
        op("G", lambda e: e.iota(out, pat, base, cm), [], w)

    def iotaf(out, pat, base, cm, w):
        op("G", lambda e: e.iota(out, pat, base, cm, allow_small_or_imprecise_dtypes=True), [], w)

    def to_next(out, in_, rs, ls):
        a = topo.addr(nxt)
        cnt[ls] = cnt.get(ls, 0) + len(topo.engines(core, nxt))
        g.remote_dma(out, in_, T.sem[rs], T.sem[ls], a[1], a[0], topo.mask(core, nxt))

    arrive = len(topo.engines(prv, core))
    smi = lambda j: T.smi[:, 24 * j:24 * j + 24]
    smf = lambda j: T.smf[:, 24 * j:24 * j + 24]

    load("S", T.ut[:], T.u[:], "lu")
    load("Y", T.xt0[:, 0:768], T.x[:, 0:768], "lx0")
    load("S", T.xt0[:, 768:1536], T.x[:, 768:1536], "lx1")
    load("Y", T.mi0[:], T.m[:], "lm")
    for t in range(1, R):
        load("Y", T["mi%d" % t][0:128 - 16 * t, :], T.m[16 * t:128, :], "lm")
        load("Y", T["mi%d" % t][128 - 16 * t:128, :], T.m[0:16 * t, :], "lm")
    wr["ut"], wr["x0a"], wr["x0b"] = [("lu", 16)], [("lx0", 16)], [("lx1", 16)]
    need("Y", wr["ut"] + wr["x0a"] + wr["x0b"])
    load("Y", T.wq[:].bitcast(dt.uint8), T.wc[:], "lw")
    load("Y", T.wp[:], T.ws[:], "lw")
    load("Y", T.vt[:], T.v[:], "lv")
    wr["vt"], wr["W"] = [("lv", 16)], [("lw", 32)]
    for t in range(R):
        wr["mi%d" % t] = [("lm", cnt["lm"])]

    iota(T.ui[:], [[16, 8]], 0, 0, ["ui"])
    iota(T.pI[:], [[0, 24]], 0, 1, ["pI"])
    iota(T.jI[:], [[16, 24]], 0, 0, ["jI"])
    iotaf(T.im16[:], [[0, 24], [1, 16]], 0, 0, ["im16"])
    fill(T.cst[:, 2048:4096], 0.0, [], ["cstC"])
    for b in range(4):
        fill(T.cst[:, 2048 + 512 * b + b:2048 + 512 * b + 512:4], 1.0, ["cstC"], ["C%d" % b])
    CC = ["cstC", "C0", "C1", "C2", "C3"]
    fun(T.cst[:, 0:1024], T.cst[:, 2048:3072], AF.Copy, CC, ["cstE0"], 0.0, 0.0)
    iotaf(T.im4[:], [[0, 96], [1, 4]], 0, 0, ["im4"])
    fill(T.ones[:], 1.0, [], ["ones"])
    for c in (slice(0, 16), slice(400, 528)):
        fill(T.fl1[:, c], 0.0, [], ["fl1", "fl1z"])
    quant(T.cq[:, 512:1024], T.cs[:, 512:1024], T.cst[:, 2048:4096], CC, ["cqC"])
    ts(T.pw[:], T.pI[:], 15, A.bitwise_and, ["pI"], ["pw"])
    copy(T.uo[:], T.ui[:], ["ui"], ["uo"])
    copy(T.tf[:, 0:1], T.pw[:, 0:1], ["pw"], ["tf0"])
    ts(T.tc[:, 0:1], T.pw[:, 0:1], 12, A.bitwise_and, ["pw"], ["tc"])
    ts(T.tf[:, 1:2], T.tc[:, 0:1], 0.25, A.mult, ["tc"], ["tf1"])
    quant(T.uq[:], T.us[:], T.ut[:], ["ut"], ["uq"])
    copy(T.ur[:, 0:128].bitcast(dt.uint32), T.uq[:, 0:128].bitcast(dt.uint32).indirect(T.uo[:, 0:8]), ["uq", "uo"], ["ur"])
    act(T.urs[:, 0:128], T.us[:, 0:128].indirect(T.uo[:, 0:8]), None, ["uq", "uo"], ["urs"])
    for k in (2, 3):
        for c in (slice(0, 16), slice(400, 528)):
            fun(T["fl%d" % k][:, c], T.fl1[:, c], AF.Copy, ["fl1"], ["fl%d" % k])
    fun(T.cst[:, 1024:2048], T.cst[:, 2048:3072], AF.Copy, CC, ["cstE1"], 0.0, 0.0)
    iotaf(T.fi[:], [[1, 384]], 0, 0, ["fi"])

    def late_calls_of_g():
        for b in range(4):
            op("G", lambda e, b=b: e.affine_select(T.cst[:, 512 * b + b:512 * b + 512:4], T.ones[:], [[-1, 128]], A.is_equal, 0.0, 0, 1),
               ["ones", "cstE0", "cstE1"], ["E%d" % b])
        iotaf(T.gi[:], [[1, 384]], 384, 0, ["gi"])

    def table(t):
        iotaf(T["wn%d" % t][:, 0:384], [[1, 384]], 0, 0, ["wna%d" % t])
        iotaf(T["wn%d" % t][:, 384:648], [[0, 264]], 768, 0, ["wnb%d" % t])

    def late_constants_1():
        fun(T.r16[:], T.im16[:], AF.Sign, ["im16"], ["r16"])
        fun(T.r4[:], T.im4[:], AF.Sign, ["im4"], ["r4"])
        for t in range(R):
            fun(T["fw%d" % t][:, 3072:3088], T.fl1[:, 0:16], AF.Copy, ["fl1z"], ["fz%d" % t])

    def late_masks():
        fun(T.ab[:], T.im16[:], AF.Abs, ["im16", "tf0"], ["ab"], T.tf[:, 0:1], -1.0)
        fun(T.k16[:], T.ab[:], AF.Relu, ["ab"], ["k16"], 1.0, -1.0)
        fun(T.ab[:], T.im4[:], AF.Abs, ["im4", "tf1"], ["ab"], T.tf[:, 1:2], -1.0)
        fun(T.k4[:], T.ab[:], AF.Relu, ["ab"], ["k4"], 1.0, -1.0)

    def late_constants_3():
        ts(T.c2[:], T.iw[:], 2.0, A.mult, ["iw"], ["c2"], 1.0, A.add)
        ts(T.tc[:, 1:2], T.pw[:, 0:1], 3, A.bitwise_and, ["pw"], ["tc1"])
        copy(T.tf[:, 2:3], T.tc[:, 1:2], ["tc1"], ["tf"])

    def inverse():
        copy(T.inv[:, 0:384].indirect(T.mu0[:, 0:24]), T.fi[:], ["fi", "mu0"], ["inv"])
        tt(T.ik[:], T.inv[:], T.k16[:], A.mult, ["inv", "k16"], ["ik"])
        scan(T.ih[:], T.r16[:], T.ik[:], 0.0, A.mult, A.add, ["r16", "ik"], ["ih"])
        copy(T.iv0[:], T.ih[:, 15:384:16], ["ih"], ["iv0"])
        need("Y", wr["iv0"])
        for t in range(1, R):
            load("Y", T["iv%d" % t][0:128 - 16 * t, :], T.iv0[16 * t:128, :], "rt")
            load("Y", T["iv%d" % t][128 - 16 * t:128, :], T.iv0[0:16 * t, :], "rt")
        for t in range(1, R):
            wr["iv%d" % t] = [("rt", cnt["rt"])]

    E = lambda b: (T.cq[:, 128 * b:128 * b + 128], T.cs[:, 128 * b:128 * b + 128])
    ONE = lambda b: (T.cq[:, 512 + 128 * b:640 + 128 * b], T.cs[:, 512 + 128 * b:640 + 128 * b])
    bank = [T["b%d" % b] for b in range(8)]
    hw = lambda k: T.ho[:, 384 * k - 369:384 * k:16]
    N = lambda k: T.nn[:, k - 1:k]

    def unpack(b, k, c, s, w, keys):
        e, es = E(b)
        mm(bank[k][:, 0:w], e, es, c, s, ["cqE"] + keys, ["B%d" % k])

    def count(k):
        quant(T.flq[:], T.fls[:], T["fl%d" % k][:, 16:528], ["fl%d" % k], ["flq"])
        for b in range(4):
            c, s = ONE(b)
            mm(bank[4 + b][:, 0:128], c, s, T.flq[:], T.fls[:], ["cqC", "flq"], ["B%d" % (4 + b)])

    def licence(k, t, between):
        for b in (0, 2):
            fun(T.lic[:, b:384:4], bank[4 + b][:, 0:96], AF.Sign, ["B%d" % (4 + b)], ["lic%d" % b], -72.0)
        for b in (1, 3):
            ts(T.lic[:, b:384:4], bank[4 + b][:, 0:96], 72.0, A.is_ge, ["B%d" % (4 + b)], ["lic%d" % b])
            if b == 1:
                between()
        tt(T["fl%d" % (k + 1)][:, 16:400], T.lic[:, 0:384].indirect(T["mu%d" % t][:, 0:24]), T.fl1[:, 16:400], A.max,
           ["lic0", "lic1", "lic2", "lic3", "mu%d" % t, "fl1"], ["fl%d" % (k + 1)])

    def prefix(k):
        f = T["fl%d" % k]
        scan(T.sc[:, 392 * k - 392:392 * k - 6], f[:, 15:401], f[:, 16:402], float(k == 3), A.add, A.add, ["fl%d" % k], ["sc%d" % k])

    def hold(k):
        scan(T.ho[:, 384 * k - 384:384 * k], T.m16[:], T.sc[:, 392 * k - 392:392 * k - 8], 0.0, A.add, A.min, ["m16", "sc%d" % k], ["ho%d" % k])

    def first_lists():
        copy(T.smi[:, 0:48], T.ho[:, 15:768:16], ["ho1", "ho2"], ["I12"])
        copy(T.nn[:, 0:2], T.sc[:, 384:1168:392], ["sc1", "sc2"], ["n12"])
        tt(smf(0), hw(2), hw(1), A.subtract, ["ho1", "ho2"], ["f2"])

    def first_bonds():
        tt(T.iw[:], T.pw[:], T.jI[:], A.add, ["pw", "jI"], ["iw"])
        copy(T.mu0[:], T.mi0[:], ["mi0"], ["mu0"])
        ts(smf(8), T.iw[:], 770.0, A.add, ["iw"], ["bi"])

    for t in range(R):
        x, xq, xs, u = T["xt%d" % t], T["xq%d" % t], T["xs%d" % t], t + 1
        fw, gq, gs = T["fw%d" % t], T["gq%d" % t], T["gs%d" % t]
        zt, zq, zs, wn = T["zt%d" % t], T["zq%d" % t], T["zs%d" % t], T["wn%d" % t]
        XQ = ["xq%d0" % t, "xq%d1" % t]
        for h in range(2):
            src = ["x0" + "ab"[h]] if t == 0 else ["x%d%s" % (t, k) for k in ("abcd", "abef")[h]]
            c = slice(192 * h, 192 * h + 192)
            quant(xq[:, c], xs[:, c], x[:, 768 * h:768 * h + 768], src, [XQ[h]])
            mm(bank[4 + h][:, 0:192], T.ur[:], T.urs[:], xq[:, c], xs[:, c], ["ur", "urs", XQ[h]], ["B%d" % (4 + h)])
        need("G", wr[XQ[1]])
        aq, sq = T["aq%d" % t], T["as%d" % t]
        to_next(sq[:], xs[:], "aq%d" % t, "lq%d" % t)
        to_next(aq[:, 0:192].bitcast(dt.uint8), xq[:, 0:192].bitcast(dt.uint8), "aq%d" % t, "lq%d" % t)
        to_next(aq[:, 192:384].bitcast(dt.uint8), xq[:, 192:384].bitcast(dt.uint8), "ar%d" % t, "lq%d" % t)
        wr["aq%d" % t] = [("aq%d" % t, 2 * arrive)]
        wr["ar%d" % t] = [("ar%d" % t, arrive)]
        if t == 0:
            late_calls_of_g()
            table(0)
            ts(T.m16[:], T.im16[:], T.tf[:, 0:1], A.is_equal, ["im16", "tf0"], ["m16"], 4096.0, A.mult)
        for h in range(2):
            ts(T.fl1[:, 16 + 192 * h:208 + 192 * h], bank[4 + h][:, 0:192], 0.0, A.is_gt, ["B%d" % (4 + h)], ["fl1"])

        def own(b):
            unpack(b, b, xq[:], xs[:], 384, XQ)
            act(fw[:, b:1536:4], bank[b][:, 0:384], None, ["B%d" % b], ["f%d%d" % (t, b)])
        count(1)
        prefix(1)
        hold(1)
        licence(1, t, first_bonds if t == 0 else lambda: None)
        if t == 0:
            late_constants_1()
        else:
            own(0)
            own(1)
        count(2)
        prefix(2)
        hold(2)
        if t == 0:
            quant(T.cq[:, 0:512], T.cs[:, 0:512], T.cst[:, 0:2048], ["cstE0", "cstE1", "E0", "E1", "E2", "E3"], ["cqE"])
        licence(2, t, first_lists)
        if t == 0:
            late_masks()
            own(0)
            own(1)
        else:
            own(2)
            own(3)
        if t == R - 1:
            fun(T.wt[:], T.fl1[:, 16:400], AF.Copy, ["fl1"], ["wt"], 4.0, -1.0)
        prefix(3)
        ts(T.smi[:, 48:96], T.smi[:, 0:48], 1, A.bitwise_and, ["I12"], ["a12"])
        hold(3)
        copy(N(3), T.sc[:, 1168:1169], ["sc3"], ["n3"])
        copy(smi(5), hw(3), ["ho3"], ["I3"])
        tt(smf(4), hw(3), hw(2), A.subtract, ["ho2", "ho3"], ["f4"])
        ts(smf(6), hw(1), N(1), A.subtract, ["ho1", "n12", "n3"], ["f6"], N(3), A.add)
        ts(smi(4), smi(5), 1, A.bitwise_and, ["I3"], ["na3"])
        ts(smf(7), smf(0), N(2), A.subtract, ["f2", "n12", "n3"], ["f7"], N(3), A.add)
        tt(T.smf[:, 24:96], T.smf[:, 144:216], T.smi[:, 48:120], A.mult, ["f6", "f7", "bi", "a12", "na3"], ["f123"])
        tt(T.smf[:, 216:264], T.smf[:, 24:72], T.smf[:, 72:120], A.max, ["f123", "f4"], ["f9"])
        tt(smf(5), smf(9), smf(10), A.max, ["f9"], ["f5"])
        copy(T["ps%d" % t][:], smf(5), ["f5"], ["ps%d" % t])
        need("G", wr["ps%d" % t])
        to_next(T["pr%d" % t][:], T["ps%d" % t][:], "ap%d" % t, "lp%d" % t)
        wr["pr%d" % t] = [("ap%d" % t, arrive)]
        if t == 0:
            table(1)
            table(2)

        for h in range(2):
            c = slice(192 * h, 192 * h + 192)
            for b in range(4):
                k = 4 * h + b
                unpack(b, k, aq[:, c], sq[:, c], 192, ["aq%d" % t, "ar%d" % t][:h + 1])
                act(T.fp[:, 768 * h + b:768 * h + 768:4], bank[k][:, 0:192], None, ["B%d" % k], ["p%d" % k])
        if t == 0:
            own(2)
            own(3)
        if t == 0:
            late_constants_3()
        tt(smi(6), T.c2[:], smi(5), A.subtract, ["c2", "I3"], ["j6"])
        tt(T["dm%d" % t][:], T.iw[:], T["mi%d" % t][:], A.subtract, ["mi%d" % t, "iw"], ["dm%d" % t])
        ts(smi(8), smi(6), 254, A.bitwise_and, ["j6"], ["j8"])
        tt(smi(7), smi(2), T["dm%d" % t][:], A.mult, ["a12", "dm%d" % t], ["j7"])
        ts(smi(10), smi(8), 386.0, A.add, ["j8"], ["j10"])
        tt(smi(9), smi(7), T["mi%d" % t][:], A.add, ["j7", "mi%d" % t], ["j9"])
        tt(smi(6), smi(10), smi(4), A.mult, ["j10", "na3"], ["j6"])
        tt(smi(11), smi(6), smi(9), A.max, ["j6", "j9"], ["j11"])
        copy(T.qu[:], smi(11), ["j11"], ["qu"])
        if t == R - 1:
            tt(T.wt[:], T.wt[:], T.fl2[:, 16:400], A.subtract, ["fl2", "wt"], ["wt"])
        for h in range(2):
            c = slice(192 * h, 192 * h + 192)
            quant(gq[:, c], gs[:, c], T.fp[:, 768 * h:768 * h + 768], ["p%d" % k for k in range(4 * h, 4 * h + 4)], ["gq%d" % h])
            for b in range(4):
                k = 4 * h + b
                unpack(b, k, gq[:, c], gs[:, c], 192, ["gq%d" % h])
                act(fw[:, 1536 + 768 * h + b:2304 + 768 * h:4], bank[k][:, 0:192], None, ["B%d" % k], ["g%d" % k])
        if u < R:
            copy(T["mu%d" % u][:], T["mi%d" % u][:], ["mi%d" % u], ["mu%d" % u])
        if t == 1:
            quant(T.vq[:], T.vs[:], T.vt[:], ["vt"], ["vq"])

        copy(wn[:, 384:1544].indirect(T["pr%d" % t][:, 0:24]), T.gi[:], ["gi", "pr%d" % t], ["wnb%d" % t])
        tt(T.lk[:], wn[:, 0:648].indirect(T.qu[:, 0:24]), T.k4[:], A.mult, ["wna%d" % t, "wnb%d" % t, "qu", "k4"], ["lk"])
        scan(T.h4[:], T.r4[:], T.lk[:], 0.0, A.mult, A.add, ["r4", "lk"], ["h4"])
        ts(T.zo[:], T.h4[:, 3:384:4], 4.0, A.mult, ["h4", "tf"], ["zo"], T.tf[:, 2:3], A.add)
        win = ["f%d%d" % (t, b) for b in range(4)] + ["g%d" % k for k in range(8)] + ["fz%d" % t, "zo"]
        P2 = (slice(0, CUT), slice(CUT, C))
        wide = (CUT, C - CUT)
        Z = ["za%d" % t, "zb%d" % t]
        for h in (0, 1):
            f4, off = slice(4 * P2[h].start, 4 * P2[h].stop), T.zo[:, P2[h].start // 4:P2[h].stop // 4]
            if h == 0 and t > 0:
                copy(zt[:, f4], fw[:, 0:3088].indirect(off), win, [Z[h]])
            else:
                act(zt[:, f4], fw[:, 0:3088].indirect(off), None, win, [Z[h]])
        if t == 0:
            inverse()
        for h in (0, 1):
            quant(zq[:, P2[h]], zs[:, P2[h]], zt[:, 4 * P2[h].start:4 * P2[h].stop], [Z[h]], ["zq%d" % h])
        ts(T.z32[:, 0:C], zt[:, 0:4 * C:4], 32.0, A.mult, Z, ["z0"])
        for b in range(1, 4):
            act(T.z32[:, C * b:C * b + C], zt[:, b:4 * C:4], 32.0, Z, ["z%d" % b])
        for b in range(4):
            for h in (0, 1):
                k = 4 * h + b
                mm(bank[k][:, 0:wide[h]], T.wq[:, 128 * b:128 * b + 128], T.wp[:, 128 * b:128 * b + 128],
                   zq[:, P2[h]], zs[:, P2[h]], ["W", "zq%d" % h], ["B%d" % k])
        if t == R - 1:
            tt(T.wx[:], T.wt[:], T.fl3[:, 16:400], A.subtract, ["wt", "fl3"], ["wx"])

        xn, iv, ivk = T["xt%d" % u], T["iv%d" % t], ["iv%d" % t]
        part = lambda b: T.tt[:, C * b:C * b + C]

        def add(b):
            for h in (0, 1):
                c, k = slice(C * b + P2[h].start, C * b + P2[h].stop), 4 * h + b
                tt(T.tt[:, c], bank[k][:, 0:wide[h]], T.z32[:, c], A.add, ["B%d" % k, "z%d" % b], ["t%d%d" % (b, h)])
        add(0)
        add(1)
        act(xn[:, 0:1536:4], part(0).indirect(iv[:, 0:24]), 0.03125, ["t00", "t01"] + ivk, ["x%da" % u])
        act(xn[:, 1:1536:4], part(1).indirect(iv[:, 0:24]), 0.03125, ["t10", "t11"] + ivk, ["x%db" % u])
        add(2)
        add(3)
        for b, k in ((2, "ce"), (3, "df")):
            tk = ["t%d0" % b, "t%d1" % b] + ivk
            ts(xn[:, b:768:4], part(b).indirect(iv[:, 0:12]), 0.03125, A.mult, tk, ["x%d%s" % (u, k[0])])
            act(xn[:, 768 + b:1536:4], part(b).indirect(iv[:, 12:24]), 0.03125, tk, ["x%d%s" % (u, k[1])])

    store("Y", T.wv[:], T.wx[0:128:16, :], ["wx"])
    x, xq, xs = T["xt%d" % R], T["xq%d" % R], T["xs%d" % R]
    K2 = ["xq%d0" % R, "xq%d1" % R]
    for h in range(2):
        c = slice(192 * h, 192 * h + 192)
        quant(xq[:, c], xs[:, c], x[:, 768 * h:768 * h + 768], ["x%d%s" % (R, s) for s in ("abcd", "abef")[h]], [K2[h]])
        mm(bank[4 + h][:, 0:192], T.vq[:], T.vs[:], xq[:, c], xs[:, c], ["vq", K2[h]], ["B%d" % (4 + h)])
        act(T.yt[:, c], bank[4 + h][:, 0:192], None, ["B%d" % (4 + h)], ["y%d" % h])
        store("Y", T.oc[:, 768 * h:768 * h + 768], xq[:, c].bitcast(dt.uint8), [K2[h]])
    store("S", T.y[:, 192:384], T.yt[:, 192:384], ["y1"])
    store("Y", T.y[:, 0:192], T.yt[:, 0:192], ["y0"])
    for k in range(4):
        store("YS"[k % 2], T.osc[4 * k:4 * k + 4, :], xs[32 * k:32 * k + 4, :], K2)
    need("G", [(s, n) for s, n in cnt.items()])
